import numpy as np, ml_dtypes
CORES = [35,38,43,46]
N = 4
import mx_ref
BF = ml_dtypes.bfloat16
def gentries(a):
    return np.ascontiguousarray(a.reshape(8, 16, -1).transpose(0, 2, 1)).reshape(8, -1)
def gtable(e):
    e = np.asarray(e); return np.ascontiguousarray(e.reshape(8, -1, 16).transpose(0, 2, 1)).reshape(128, -1).astype(np.int32)
def gcols(t, e):
    v = np.concatenate([t.reshape(8, 16, -1, 4), np.zeros((8, 16, 1, 4), BF)], axis=2)
    return np.ascontiguousarray(np.stack([v[g][:, e[g]] for g in range(8)])).reshape(128, -1)
def gpick(z, e):
    return np.concatenate([z[16 * g:16 * g + 16][:, e[g]] for g in range(8)])
def tile(rs):
    return np.stack(rs, axis=2).reshape(128, -1).astype(BF)
def pick(q, e):
    c = np.concatenate([q[0].reshape(128, -1, 4), np.zeros((128, 1, 4), np.uint8)], axis=1); s = np.concatenate([q[1], np.ones((16, 1), np.uint8)], axis=1)
    return (np.ascontiguousarray(c[:, e].reshape(128, -1)), np.ascontiguousarray(s[:, e]))
def join(*qs):
    return (np.concatenate([q[0] for q in qs], axis=1), np.concatenate([q[1] for q in qs], axis=1))
def put(q, e, v):
    c, s = q[0].reshape(128, -1, 4).copy(), q[1].copy(); c[:, e] = v[0].reshape(128, -1, 4); s[:, e] = v[1]
    return (c.reshape(128, -1), s)
def pk(c, s):
    return (np.ascontiguousarray(c), mx_ref.live(s))
def emit(q):
    return q[0], q[1]
def packed(v, rng):
    q = [mx_ref.quantize(np.ascontiguousarray(v[r])) for r in range(N)]
    return np.stack([a for a, b in q]), np.stack([mx_ref.plane(b, rng) for a, b in q])
def values_of_codes():
    e, c = np.zeros((128, 128, 4), np.float32), np.zeros((128, 2, 4), np.uint8)
    e[np.arange(128), np.arange(128), 0] = 1
    c[:127, :, 0] = np.arange(256).reshape(2, 128).T[:127]
    return mx_ref.matmul(mx_ref.quantize(e.reshape(128, 512).astype(BF)), (c.reshape(128, 8), np.full((16, 2), 127, np.uint8))).T.reshape(-1).astype(np.float64)
CODE_VALUE, SCALE_VALUE = values_of_codes(), 2.0 ** (np.arange(256) - 127.0)
def decode(q):
    return (CODE_VALUE[q[0]].reshape(16, 8, -1, 4) * SCALE_VALUE[q[1]][:, None, :, None] + 0.0).reshape(128, -1).astype(np.float32)
def f(rng, *shape):
    return mx_ref.flush((rng.standard_normal(shape, dtype=np.float32) * np.exp2(rng.integers(-2, 3, shape[:-1] + (1,)))).astype(BF))
def wide(rng, *shape, cols=0):
    v = rng.standard_normal(shape, dtype=np.float32) * np.exp2(rng.integers(-12, 13, shape)).astype(np.float32)
    if cols: v *= np.repeat(np.exp2(rng.integers(-cols, cols + 1, shape[:-2] + (1, shape[-1] // 4))) * (rng.random(shape[:-2] + (1, shape[-1] // 4)) > 0.0625), 4, axis=-1).astype(np.float32)
    return mx_ref.flush(v.astype(BF))
C = 384
STEP = [2, 3, 1]
def numbers_of(rng):
    return {"x": np.array(f(rng, N, 128, 4 * C)), "u": np.array(f(rng, N, 128, 512)), "v": np.array(f(rng, N, 128, 512))}
def orders(rng):
    return rng.permuted(np.tile(np.arange(C), (N, 8, 1)), axis=2), rng.permuted(np.tile(np.arange(8)[:, None], (N, 1, C)), axis=1)
def stored(p, o):
    return {"pg": np.stack([gtable(p[r]) for r in range(N)]), "og": np.stack([gtable(o[r]) for r in range(N)])}
def layers(rng, still=[]):
    w = np.array(f(rng, N, 128, 2048)).reshape(N, 8, 16, 4, 8, 16, 4)
    for i in still:
        w[:, :, i] = 0
        w[:, :, :, :, :, i] = 0
    return w
def weights(rng, w):
    c, s = packed(np.ascontiguousarray(w).reshape(N, 128, 2048), rng)
    return {"wc": c, "ws": s}
def setup_inputs(rng):
    return {**numbers_of(rng), **stored(*orders(rng)), **weights(rng, layers(rng))}
def setup_inputs_ties(rng):
    d = numbers_of(rng)
    n = rng.permutation(N)
    k = rng.integers(0, 4, (N, 8, C))
    k[n[1]] -= 4
    k[n[2]] = np.arange(8)[:, None]
    x = d["x"].reshape(N, 8, 16, C, 4)
    x[:, :, 0] = 0
    x[:, :, 0, :, 0] = k.astype(np.float32).astype(BF)
    u = d["u"].reshape(N, 128, 128, 4)
    u[:, :, ::16] = 0
    for r in range(N):
        for h in range(0, 128, 16): u[r, h, h, 0] = 0.0 if r == n[0] else 1.0
    p, o = orders(rng)
    o[n[2]] = 7 - np.arange(8)[:, None]
    return {"x": x.reshape(N, 128, 4 * C), "u": u.reshape(N, 128, 512), "v": d["v"], **stored(p, o), **weights(rng, layers(rng, [0]))}
def setup_inputs_near(rng):
    d = numbers_of(rng)
    x = d["x"].astype(np.float32).reshape(N, 8, 16, C, 4)
    x[:, :, 0] = 0
    x[:, :, 8:] = 0
    u = d["u"].reshape(N, 128, 128, 4)
    u[:, :, ::16] = 0
    w = layers(rng, [0, 8, 9, 10, 11, 12, 13, 14, 15])
    kind, size, least = np.zeros(N, np.int64), np.ones(N), 2.0 ** -30
    turn = rng.integers(2)
    for i, r in enumerate(rng.permutation([r for r in range(N) if r < r ^ STEP[0]])):
        both = [r, r ^ STEP[0]]
        kind[both] = 2 if i == 0 else rng.permutation(2)
        size[both] = least if (i + turn) % 2 else 1.0
    for r in range(N):
        s = rng.integers(0, 16, (8, C))
        digits = ((s[:, :, None] >> np.arange(4)) & 1) * np.exp2(np.arange(4) - 23.0)
        if kind[r] == 0:
            x[r, :, 0, :, 0] = rng.choice([-1.0, 1.0])
            x[r, :, 8] = digits
            x[r, :, 11, :, 0] = 2.0 ** -10
        if kind[r] == 1: x[r, :, 8] = digits * rng.choice([-1.0, 1.0], (8, C, 1))
        if kind[r] == 2:
            e = rng.integers(-1, 2, (8, C)) * least
            x[r, :, 8, :, 0] = 1.25 * e
            x[r, :, 9, :, 0] = -1.125 * e
            x[r, :, 13, :, 0] = rng.choice([-1.0, 1.0], (8, C)) * least
            for g in range(8): w[r, g, 13, 0, g, 12, 0] = 2.0 ** -8
        for g, j in zip(rng.permutation(8)[:4], [0, C - 1, int(rng.integers(C)), int(rng.integers(C))]): x[r, g, 0, j, 0] = 2.0 ** 29 * rng.choice([-1.0, 1.0])
        k = size[r] if kind[r] == 0 else least
        for h in range(0, 128, 16):
            u[r, h, h, 0] = k if kind[r] == 0 else 1.0
            if kind[r] == 0: u[r, h + 11, h, 0] = k
            if kind[r] < 2: u[r, h + 8, h] = k
            else:
                u[r, h + 8, h, 0] = k
                u[r, h + 9, h, 0] = 1.125 * k
                u[r, h + 12, h, 0] = k
    return {"x": x.reshape(N, 128, 4 * C).astype(BF), "u": u.reshape(N, 128, 512), "v": d["v"], **stored(*orders(rng)), **weights(rng, w)}
def setup_inputs_odd(rng):
    d = numbers_of(rng)
    x = (1.0 + (2 * rng.integers(0, 64, (N, 16, 8, C, 4)) + 1) * 2.0 ** -7) * np.exp2(-rng.integers(0, 7, (N, 16, 8, C, 4)).astype(np.float64)) * rng.choice([-1.0, 1.0], (N, 16, 8, C, 4))
    x[:, :, 0, :, 0] = 1.96875 * 2.0 ** 8 * rng.choice([-1.0, 1.0], (16, 1))
    u = d["u"].reshape(N, 16, 8, 128, 4)
    u[:, :, 0, ::16] = 0
    w = layers(rng, [0, 8])
    for g in range(8):
        for i in (0, 8): w[:, g, i, 0, g, i, 0] = -0.5
    return {"x": x.astype(np.float32).reshape(N, 128, 4 * C).astype(BF), "u": u.reshape(N, 128, 512), "v": d["v"], **stored(*orders(rng)), **weights(rng, w)}
def setup_inputs_ends(rng):
    d = numbers_of(rng)
    n, e, c = [rng.permutation(N) % 4 for _ in range(3)]
    low, tiny = 2.0 ** 29, 2.0 ** -30
    def small(*s): return (1 + 0.125 * rng.integers(0, 8, s)) * tiny
    x = np.zeros((N, 8, 16, C, 4))
    u = d["u"].astype(np.float32).reshape(N, 8, 16, 128, 4)
    v = d["v"].astype(np.float32)
    w = np.zeros((N, 128, 4, 128, 4), np.float32)
    i = np.arange(128)
    p, o = orders(rng)
    for r in range(N):
        h = rng.permutation(8)
        a = np.where(h < 2, 0.0, h % 2 * 2.0 - 1.0)[:, None]
        k = np.full(16, 4.0)
        k[15] = 0
        if n[r] < 2:
            x[r] = -(1 + 0.125 * rng.integers(0, 4, (8, 16, C, 4))) * low
            if n[r] == 1: x[r] *= rng.choice([-1.0, 1.0], (C, 1))
            x[r, :, 15] = 2.0 ** 16 * rng.choice([-1.0, 1.0], (8, C, 4))
            u[r, :, :, ::16] = a * 2.0 ** 30
            v[r] = rng.choice([-1.0, 1.0], (128, 512)) * (1 + 0.125 * rng.integers(4, 9, (128, 512))) * low
        elif n[r] == 2:
            x[r] = -small(8, 16, C, 4)
            u[r, :, :, ::16] = a * small(8, 16, 8, 4)
            u[r, :, 14:, ::16] = 0
            v[r] = rng.choice([-1.0, 1.0], (128, 512)) * small(128, 512)
            k[:] = 0
            k[14], k[15] = 2.0 ** -8, 2.0 ** 8
        else:
            x[r] = d["x"][r].astype(np.float32).reshape(8, 16, C, 4)[:, :, :1]
            u[r, :, :, ::16] *= np.abs(a).astype(np.float32)
        for b in range(4): w[r, i, b, i, b] = np.tile(k, 8)
        if e[r] < 3: p[r] = [np.arange(C), np.arange(C)[::-1], (np.arange(C) + 1) % C][e[r]]
        up = np.arange(8)[:, None]
        if c[r] < 3: o[r] = np.where([np.ones(C, bool), np.zeros(C, bool), rng.random(C) < 0.5][c[r]], up, 7 - up)
    return {"x": x.astype(np.float32).reshape(N, 128, 4 * C).astype(BF), "u": u.reshape(N, 128, 512).astype(BF), "v": v.astype(BF), **stored(p, o), **weights(rng, w.astype(BF))}
def setup_inputs_spread(rng):
    d = setup_inputs(rng)
    d["x"] = wide(rng, N, 128, 4 * C, cols=6)
    return d
def check_inputs(d):
    b = []
    for k in ("x", "u", "v"):
        a = np.abs(d[k].astype(np.float32))
        if not (np.isfinite(a).all() and ((a == 0) | (a >= 2.0 ** -30) & (a <= 2.0 ** 30)).all()): b.append("a value of " + k)
    none, least, most = [emit(mx_ref.quantize(np.full((128, 16), k, np.float32).astype(BF)))[1][0, 0] for k in (0.0, 2.0 ** -8, 2.0 ** 8)]
    for r in range(N):
        if not (np.sort(gentries(d["pg"][r]), axis=1) == np.arange(C)).all(): b.append("pg: a group's entries aren't all columns")
        if not (np.sort(gentries(d["og"][r]), axis=0) == np.arange(8)[:, None]).all(): b.append("og: a column's entries aren't all groups")
        if ((d["wc"][r] == 0x7F) | (d["wc"][r] == 0xFF)).any(): b.append("wc: a code that is no number")
        s = mx_ref.live(d["ws"][r])
        if ((s != none) & ((s < least) | (s > most))).any(): b.append("ws: a scale out of range")
        if (((d["wc"][r].reshape(16, 8, 512, 4) & 0x7F) != 0) & (s == none)[:, None, :, None]).any(): b.append("wc: a code other than zero under the scale of zeros")
    return b
def walk(p, o):
    a, at = np.arange(C), np.zeros((8, C), np.int64)
    for k in range(8):
        a = p[o[k], a]
        at[o[k], np.arange(C)] = a
    return at
def reference(x, u, v, pg, og, wc, ws):
    qu = [mx_ref.quantize(u[r]) for r in range(N)]
    lay = [pk(wc[r], ws[r]) for r in range(N)]
    p, o = [np.array(gentries(pg[r])) for r in range(N)], [np.array(gentries(og[r])) for r in range(N)]
    at = [walk(p[r], o[r]) for r in range(N)]
    now = [x[r] for r in range(N)]
    for t, step in enumerate(STEP):
        held, z = [], []
        for r in range(N):
            q = mx_ref.quantize(now[r])
            held.append(decode(q))
            s = mx_ref.matmul(qu[r], q)[::16]
            c = s[o[r], at[r][o[r], np.arange(C)]]
            for k in range(t % 2, 7, 2):
                turn = c[k] > c[k + 1]
                o[r][k], o[r][k + 1] = np.where(turn, o[r][k + 1], o[r][k]), np.where(turn, o[r][k], o[r][k + 1])
            at[r] = walk(p[r], o[r])
            z.append(mx_ref.quantize(gcols(held[r].astype(BF), at[r])))
        for r in range(N):
            e = np.take_along_axis(p[r], at[r], axis=1)
            now[r] = tile([held[r][:, b::4] + gpick(mx_ref.matmul(pick(lay[r], np.arange(128 * b, 128 * b + 128)), z[r ^ step]) * np.float32(0.03125), e) for b in range(4)])
    y, ol = np.zeros((N, 128, C), np.float32), np.zeros((N, 8, C), np.float32)
    oc, osc = np.zeros((N, 128, 4 * C), np.uint8), np.zeros((N, 16, C), np.uint8)
    for r in range(N):
        q = mx_ref.quantize(now[r])
        y[r] = mx_ref.matmul(mx_ref.quantize(v[r]), q)
        ol[r] = o[r]
        oc[r], osc[r] = emit(q)
    return {"y": y, "ol": ol, "oc": oc, "osc": osc}

@@ -1,0 +1,547 @@
+import numpy as np
+from concourse.mybir import dt, AluOpType, ActivationFunctionType
+
+C = 384
+STEP = [2, 3, 1]
+NW = 512
+BASE = 8
+TW = BASE + 8 * NW
+OP = AluOpType
+COPY = ActivationFunctionType.Copy
+F32, BF, I32, U16, X4, U8 = "float32", "bfloat16", "int32", "uint16", "float8_e4m3fn_x4", "uint8"
+
+
+def _scratch():
+    s = {}
+
+    def sb(name, shape, d):
+        s[name] = ("sbuf", [128] + shape, d)
+    sb("pgi", [24], I32); sb("ogi", [24], I32); sb("pidx", [1], I32); sb("ti", [8], I32); sb("t24", [24], I32); sb("t24b", [24], I32)
+    sb("selu", [10], U16); sb("win", [16], F32); sb("wini", [16], I32)
+    sb("pgf", [32], F32); sb("pgt", [32], F32); sb("ogf", [32], F32); sb("ogt", [32], F32)
+    sb("cst", [16], F32); sb("one16", [16], F32); sb("js", [4], F32); sb("mk8", [32], F32); sb("jbm", [8], F32)
+    sb("ones", [512], BF); sb("ebt", [2048], BF); sb("ec", [512], X4); sb("ep", [512], U8)
+    sb("xb", [4 * C], BF); sb("ub", [512], BF); sb("vb16", [512], BF)
+    sb("uq0", [128], X4); sb("up0", [128], U8); sb("uc", [160], X4); sb("upl", [160], U8)
+    sb("vq", [128], X4); sb("vp", [128], U8); sb("wcod", [512], X4); sb("wpl", [512], U8)
+    sb("tab", [TW], F32); sb("sct", [8 * NW], F32)
+    for r in range(4):
+        sb("qc%d" % r, [C], X4); sb("qp%d" % r, [C], U8)
+        if r:
+            sb("xs%d" % r, [4 * C], BF)
+    for r in range(3):
+        sb("lc%d" % r, [C], X4); sb("lp%d" % r, [C], U8); sb("zl%d" % r, [24], U16); sb("al%d" % r, [24], U16)
+        sb("zc%d" % r, [C], X4); sb("zp%d" % r, [C], U8); sb("zt%d" % r, [4 * C], BF)
+    sb("fb", [4 * C], BF); sb("dp", [4 * C], BF); sb("rs", [4 * C], F32)
+    sb("oxd", [64], F32); sb("oxw", [256], F32); sb("ox", [4, 2, 32], F32)
+    sb("oe", [32], F32); sb("oo", [32], F32)
+    sb("dd", [32], F32); sb("dd2", [32], F32); sb("d0", [8], F32); sb("mm", [32], F32); sb("mm2", [32], F32); sb("m0", [8], F32)
+    sb("idxf", [64], F32); sb("idxu", [64], U16); sb("dv", [32], F32); sb("off0", [8], F32)
+    sb("offu", [64], U16); sb("wk", [1024], F32); sb("tt", [1024], F32); sb("rep", [1024], F32)
+    sb("vs", [32], F32); sb("vadr", [32], F32); sb("eb", [32], U16)
+    sb("ev", [512], F32); sb("bt", [256], BF); sb("bd", [16, 2, 16], BF); sb("btt", [512], BF)
+    sb("brep", [512], F32); sb("brt", [512], F32); sb("lb", [32], F32)
+    for k in ("A", "B"):
+        sb("lt" + k, [32], F32); sb("xd" + k, [64], F32); sb("xw" + k, [192], F32); sb("xx" + k, [192], F32)
+        sb("cl" + k, [6, 32], F32); sb("s1" + k, [6, 16], F32); sb("s2" + k, [6, 8], F32); sb("s3" + k, [6, 4], F32)
+    sb("b5", [3, 2, 2, 2], F32); sb("bl", [24], U16)
+    sb("olf", [32], F32); sb("olg", [32], F32); sb("olt", [32], F32); sb("ys", [C], F32)
+    s["ps"] = ("psum", [128, 4096], F32)
+    return s
+
+
+SCRATCH = _scratch()
+SEMAPHORES = (["qv", "qs", "qt", "qg", "loc", "d_pg", "d_og", "d_x", "d_u", "d_w", "d_v", "d_t", "d_o", "d_ol", "d_y"]
+              + ["rq%d" % r for r in range(3)] + ["ra%d" % r for r in range(3)])
+
+
+def make_queue_tools(g, T):
+    eng = {"v": g.vector, "s": g.scalar, "t": g.tensor, "g": g, "y": g.sync}
+    own = {"v": "qv", "s": "qs", "t": "qt", "g": "qg"}
+    count = {k: 0 for k in SEMAPHORES}
+    known = {k: {} for k in eng}
+    clock = {}
+    hist = {}
+    bits = {}
+
+    def region(ref):
+        name, idx = ref
+        key = (name, str(idx))
+        if key not in bits:
+            if name == "ps":
+                bits[key] = (0, 128, 1 << idx)
+            else:
+                shape = SCRATCH[name][1][1:]
+                n = 1
+                for k in shape:
+                    n *= k
+                a = np.arange(n).reshape(shape)
+                sel = np.zeros(n, np.uint8)
+                sel[a[idx[1:]].reshape(-1)] = 1
+                m = int.from_bytes(np.packbits(sel, bitorder="little").tobytes(), "little")
+                bits[key] = (idx[0].start or 0, idx[0].stop or 128, m)
+        return bits[key]
+
+    def learn(q, ev):
+        k = known[q]
+        for s, n in clock[ev].items():
+            if k.get(s, 0) < n:
+                k[s] = n
+
+    def need(q, events):
+        todo = [e for e in set(events) if known[q].get(e[0], 0) < e[1]]
+        todo = [e for e in todo if not any(f != e and clock[f].get(e[0], 0) >= e[1] for f in todo)]
+        for e in sorted(todo):
+            if known[q].get(e[0], 0) < e[1]:
+                eng[q].wait_ge(T.sem[e[0]], e[1])
+                learn(q, e)
+
+    def deps(q, ins, outs):
+        ev = []
+        for refs, write in ((ins, False), (outs, True)):
+            for ref in refs:
+                p0, p1, m = region(ref)
+                for (h0, h1, hm, hw, hq, he) in hist.get(ref[0], ()):
+                    if (hw or write) and h0 < p1 and p0 < h1 and hm & m:
+                        if not hw and hq == q:
+                            continue
+                        ev.append(he)
+        return ev
+
+    def note(q, ev, ins, outs):
+        for refs, write in ((ins, False), (outs, True)):
+            for ref in refs:
+                p0, p1, m = region(ref)
+                lst = hist.setdefault(ref[0], [])
+                if write:
+                    lst[:] = [h for h in lst if not (p0 <= h[0] and h[1] <= p1 and (h[2] & ~m) == 0)]
+                lst.append((p0, p1, m, write, q, ev))
+
+    def op(q, call, outs, ins):
+        need(q, deps(q, ins, outs))
+        sem = own[q]
+        count[sem] += 1
+        ev = (sem, count[sem])
+        call().then_inc(T.sem[sem], 1)
+        clock[ev] = dict(known[q])
+        clock[ev][sem] = count[sem]
+        note(q, ev, ins, outs)
+
+    def dmas(sem, items):
+        count[sem] += 16 * len(items)
+        ev = (sem, count[sem])
+        clock[ev] = {sem: count[sem]}
+        for q, out, in_, outs, ins in items:
+            need(q, [e for e in deps(q, ins, outs) if e != ev])
+            eng[q].dma_start(out, in_).then_inc(T.sem[sem], 16)
+            for s, n in known[q].items():
+                if clock[ev].get(s, 0) < n:
+                    clock[ev][s] = n
+        for q, out, in_, outs, ins in items:
+            note("dma", ev, ins, outs)
+
+    def send(call, ins, n):
+        need("g", deps("g", ins, []))
+        call()
+        count["loc"] += n
+        clock[("loc", count["loc"])] = {"loc": count["loc"]}
+
+    def arrives(sem, n, outs):
+        count[sem] += n
+        ev = (sem, count[sem])
+        clock[ev] = {sem: count[sem]}
+        note("remote", ev, [], outs)
+
+    def finish():
+        for s in SEMAPHORES:
+            if count[s] and known["g"].get(s, 0) < count[s]:
+                g.wait_ge(T.sem[s], count[s])
+    return op, dmas, send, arrives, finish
+
+
+def rank_program(g, core, T, topo):
+    rank = T.rank_of(core)
+    if rank is None:
+        return
+    op, dmas, send, arrives, finish = make_queue_tools(g, T)
+    S_ = slice
+    ANY = slice(None)
+
+    def R(name, *idx, p=slice(0, 128)):
+        return (name, (p,) + tuple(idx)) if idx else (name, (p,) + tuple(ANY for _ in SCRATCH[name][1][1:]))
+
+    def V(ref):
+        return T[ref[0]][ref[1]]
+
+    def bank(k, n):
+        return T.ps[:, 512 * k:512 * k + n]
+
+    def cp(q, out, in_, scale=None):
+        if q == "v":
+            op(q, lambda: g.vector.tensor_copy(V(out), V(in_)), [out], [in_])
+        elif scale is None:
+            op(q, lambda: g.scalar.activation(V(out), V(in_), COPY), [out], [in_])
+        else:
+            op(q, lambda: g.scalar.activation(V(out), V(in_), COPY, scale=V(scale)), [out], [in_, scale])
+
+    def frombank(q, out, k, n=C, scale=None):
+        if q == "v" and scale is None:
+            op(q, lambda: g.vector.tensor_copy(V(out), bank(k, n)), [out], [("ps", k)])
+        elif q == "v":
+            op(q, lambda: g.vector.tensor_scalar(V(out), bank(k, n), scale, None, OP.mult), [out], [("ps", k)])
+        elif scale is None:
+            op(q, lambda: g.scalar.activation(V(out), bank(k, n), COPY), [out], [("ps", k)])
+        else:
+            op(q, lambda: g.scalar.activation(V(out), bank(k, n), COPY, scale=scale), [out], [("ps", k)])
+
+    def gather(q, out, win, off):
+        if q == "v":
+            op(q, lambda: g.vector.tensor_copy(V(out), V(win).indirect(V(off))), [out], [win, off])
+        else:
+            op(q, lambda: g.scalar.activation(V(out), V(win).indirect(V(off)), COPY), [out], [win, off])
+
+    def gather_add(out, win, off, in1):
+        op("v", lambda: g.vector.tensor_tensor(V(out), V(win).indirect(V(off)), V(in1), OP.add), [out], [win, off, in1])
+
+    def tt(out, a, b, o):
+        op("v", lambda: g.vector.tensor_tensor(V(out), V(a), V(b), o), [out], [a, b])
+
+    def ts(out, a, s1, s2, o0, o1=None):
+        v1 = V(s1) if isinstance(s1, tuple) else s1
+        v2 = V(s2) if isinstance(s2, tuple) else s2
+        ins = [a] + [s for s in (s1, s2) if isinstance(s, tuple)]
+        if o1 is None:
+            op("v", lambda: g.vector.tensor_scalar(V(out), V(a), v1, None, o0), [out], ins)
+        else:
+            op("v", lambda: g.vector.tensor_scalar(V(out), V(a), v1, v2, o0, o1), [out], ins)
+
+    def tr(out, in_):
+        op("v", lambda: g.vector.transpose(V(out), V(in_)), [out], [in_])
+
+    def ms(out, c):
+        op("v", lambda: g.vector.memset(V(out), c), [out], [])
+
+    def quant(oc_, op_, in_):
+        op("v", lambda: g.vector.quantize_mx(V(oc_), V(op_), V(in_)), [oc_, op_], [in_])
+
+    def mm(k, lc, lp, rc, rp, n=C):
+        op("t", lambda: g.tensor.matmul_mx(bank(k, n), V(lc), V(lp), V(rc), V(rp), True, True), [("ps", k)], [lc, lp, rc, rp])
+
+    def iota(out, pattern, base, cm, **kw):
+        op("g", lambda: g.iota(V(out), pattern, base, cm, **kw), [out], [])
+
+    def quadrant(a):
+        return slice(32 * a, 32 * a + 32)
+
+    def cols(name, a, n):
+        return R(name, S_(a, a + n))
+
+    def partner(r):
+        return T.cores[rank ^ STEP[r]]
+
+    def ways(src, dst):
+        return topo.engines(src, dst)[:8]
+
+    def remote(r, out, in_, sem, ins):
+        rid, pid, _ = topo.addr(partner(r))
+        e = ways(core, partner(r))
+        send(lambda: g.remote_dma(out, in_, T.sem[sem], T.sem.loc, pid, rid, sum(1 << k for k in e)), ins, len(e))
+
+    def q_of(r, a=0, n=C):
+        return cols("qc%d" % r, a, n), cols("qp%d" % r, a, n)
+
+    def send_state(r):
+        remote(r, T["lc%d" % r][:].bitcast(dt.uint8), T["qc%d" % r][:].bitcast(dt.uint8), "rq%d" % r, [R("qc%d" % r)])
+        remote(r, T["lp%d" % r][:], T["qp%d" % r][:], "rq%d" % r, [R("qp%d" % r)])
+
+    for r in range(3):
+        n = len(ways(partner(r), core))
+        arrives("rq%d" % r, 2 * n, [R("lc%d" % r), R("lp%d" % r)])
+        arrives("ra%d" % r, n, [R("zl%d" % r)])
+
+    dmas("d_pg", [("y", T.pgi[:], T.pg[:], [R("pgi")], [])])
+    dmas("d_og", [("s", T.ogi[:], T.og[:], [R("ogi")], [])])
+    dmas("d_x", [("y", T.xb[:], T.x[:], [R("xb")], [])])
+    dmas("d_u", [("s", T.ub[:], T.u[:], [R("ub")], [])])
+
+    def c1(k):
+        return cols("cst", k, 1)
+
+    def ti(k):
+        return cols("ti", k, 1)
+    iota(R("pidx"), [[0, 1]], 0, 1)
+    iota(R("wini"), [[NW, 16]], -8 * NW, 0)
+    ms(R("ones"), 1.0)
+    ms(cols("tab", 0, 1024), 0.0)
+    for k in (TW - 2048, TW - 1024):
+        cp("s", cols("tab", k, 1024), cols("tab", 0, 1024))
+    ms(cols("tab", 1024, TW - 3072), 0.0)
+    for b in range(4):
+        o = cols("ebt", 512 * b, 512)
+        op("g", lambda: g.affine_select(V(o), T.ones[:], [[-1, 512]], OP.is_equal, 0.0, b, 4), [o], [R("ones")])
+    ts(ti(0), R("pidx"), 4, 1, OP.arith_shift_right, OP.bitwise_and)
+    ts(ti(1), R("pidx"), 5, None, OP.arith_shift_right)
+    ms(R("pgf"), 0.0)
+    ts(c1(2), ti(0), 4.0, None, OP.mult)
+    ts(ti(2), R("pidx"), 15, None, OP.bitwise_and)
+    tt(c1(3), c1(2), ti(1), OP.add)
+    ms(R("ogf"), 0.0)
+    ts(c1(4), c1(3), float(NW), float(BASE), OP.mult, OP.add)
+
+    ts(cols("pgf", 0, 24), R("pgi"), c1(4), None, OP.add)
+    tr(R("pgt"), R("pgf"))
+    items = []
+    for G in range(6):
+        for h in range(2):
+            a, n = BASE + 4 * NW * h, 4 * NW
+            pr = slice(16 * G, 16 * G + 1)
+            items.append((("y", "s")[h], T.tab[pr, a:a + n], T.pgt[:, 16 * h:16 * h + 16],
+                          [R("tab", S_(a, a + n), p=pr)], [cols("pgt", 16 * h, 16)]))
+    dmas("d_t", items)
+    dmas("d_w", [("y", T.wcod[:].bitcast(dt.uint8), T.wc[:], [R("wcod")], []), ("y", T.wpl[:], T.ws[:], [R("wpl")], [])])
+    dmas("d_v", [("y", T.vb16[:], T.v[:], [R("vb16")], [])])
+
+    ts(R("t24"), R("ogi"), 1, None, OP.bitwise_and)
+    ts(R("t24b"), R("ogi"), 1, None, OP.arith_shift_right)
+    ts(R("t24"), R("t24"), 4.0, None, OP.mult)
+    ms(R("one16"), 1.0)
+    tt(cols("ogf", 0, 24), R("t24"), R("t24b"), OP.add)
+    ts(ti(3), R("pidx"), 1, 3, OP.arith_shift_right, OP.bitwise_and)
+    tr(R("ogt"), R("ogf"))
+
+    def spread(src, xd, xw, nsrc):
+        for H in range(2):
+            for h in range(2):
+                cp("vs"[H], cols(xd, 32 * h + 16 * H, 16), cols(src, 16 * h, 16))
+        k = 0
+        for a in range(nsrc):
+            for b in range(4):
+                cp("vs"[k % 2], R(xw, S_(64 * a, 64 * a + 64), p=quadrant(b)), R(xd, p=quadrant(a)))
+                k += 1
+
+    spread("ogt", "oxd", "oxw", 4)
+    quant(*q_of(0), R("xb"))
+    send_state(0)
+    for x in range(8):
+        iota(cols("sct", NW * x + C, NW - C), [[0, NW - C]], 0, 0, allow_small_or_imprecise_dtypes=True)
+    ts(ti(4), R("pidx"), 3, 1, OP.arith_shift_right, OP.bitwise_and)
+    cp("v", c1(1), ti(0))
+    ts(c1(9), ti(3), 32.0, None, OP.mult)
+    ts(c1(10), ti(4), 16.0, None, OP.mult)
+    tr(R("ox"), R("oxw"))
+    tt(c1(9), c1(9), c1(10), OP.add)
+    ts(c1(0), ti(0), -1.0, 1.0, OP.mult, OP.add)
+    ts(R("selu"), cols("one16", 0, 10), c1(9), None, OP.mult)
+    quant(R("uq0"), R("up0"), R("ub"))
+    op("v", lambda: g.vector.tensor_copy(T.uc[:].bitcast(dt.uint32), T.uq0[:].bitcast(dt.uint32).indirect(T.selu[:])),
+       [R("uc")], [R("uq0"), R("selu")])
+    op("s", lambda: g.scalar.activation(T.upl[:], T.up0[:].indirect(T.selu[:]), COPY), [R("upl")], [R("up0"), R("selu")])
+    for par, name in ((0, "oe"), (1, "oo")):
+        for a in range(4):
+            for h in range(2):
+                o = R(name, S_(h, 32, 2), p=quadrant(a))
+                i = R("ox", ANY, par, S_(8 * a + 4 * h, 8 * a + 4 * h + 4), p=quadrant(a))
+                s = R("cst", S_(h, h + 1), p=quadrant(a))
+                if par:
+                    cp("s", o, i, s)
+                else:
+                    ts(o, i, s, None, OP.mult)
+    oe, oo, mk8 = R("oe"), R("oo"), R("mk8")
+    IE, IO = cols("idxf", 0, 32), cols("idxf", 32, 24)
+    for h in range(2):
+        ts(R("mk8", S_(h, 32, 2)), R("one16"), c1(h), 8.0, OP.mult, OP.mult)
+    ts(c1(7), ti(1), 128.0, None, OP.mult)
+    ts(c1(8), ti(0), 64.0, None, OP.mult)
+    cp("v", R("win"), R("wini"))
+    tt(c1(7), c1(7), c1(8), OP.add)
+    cp("v", cols("idxf", 56, 8), cols("mk8", 0, 8))
+    tt(c1(7), c1(7), ti(2), OP.add)
+    ms(cols("win", 0, 1), 0.0)
+    tt(R("dd"), oo, oe, OP.subtract)
+    tt(IO, cols("oe", 8, 24), cols("oo", 0, 24), OP.subtract)
+    tt(IE, R("dd"), mk8, OP.add)
+    tt(IO, IO, cols("mk8", 0, 24), OP.add)
+    for s in range(4):
+        ts(cols("js", s, 1), c1(7), 16.0 * s + BASE, None, OP.add)
+    cp("v", R("idxu"), R("idxf"))
+    ts(R("off0"), cols("oe", 0, 8), float(NW), None, OP.mult)
+    for h in range(2):
+        ts(R("jbm", S_(h, 8, 2)), R("js"), c1(h), None, OP.mult)
+    tt(R("off0"), R("off0"), R("jbm"), OP.add)
+    cp("v", cols("offu", 0, 8), R("off0"))
+
+    KAP = [0, 4, 1, 5, 2, 6, 3, 7]
+
+    def rep(k):
+        gather("s", cols("rep", 128 * KAP[k], 128), R("win"), cols("idxu", 8 * KAP[k], 8))
+
+    def walk(first, fill):
+        for k in range(first, 8):
+            z = KAP[k]
+            blk, off = (128 * z, 128), cols("offu", 8 * z, 8)
+            if k < 7:
+                gather_add(cols("wk", *blk), R("tab"), off, cols("rep", *blk))
+            else:
+                gather("v", cols("wk", *blk), R("tab"), off)
+            for f in fill.pop((k, 0), ()):
+                f()
+            tr(cols("tt", *blk), cols("wk", *blk))
+            for f in fill.pop((k, 1), ()):
+                f()
+            if k < 7:
+                cp("v", cols("offu", 8 * KAP[k + 1], 8), R("tt", S_(128 * z, 128 * z + 128, 16)))
+
+    def dv_fill(fill):
+        fill.setdefault((4, 1), []).append(lambda: tt(R("dv"), R("idxf", S_(0, 64, 2)), R("idxf", S_(1, 64, 2)), OP.add))
+        fill.setdefault((5, 1), []).append(lambda: ts(R("dv"), R("dv"), -float(NW), 8.0 * NW, OP.mult, OP.add))
+        return fill
+
+    def addresses():
+        tt(R("vs"), R("tt", S_(0, 1024, 32)), R("tt", S_(16, 1024, 32)), OP.add)
+        tt(R("vadr"), R("vs"), R("dv"), OP.add)
+
+    def list_of_addresses():
+        ts(R("eb"), R("vadr"), -float(BASE), None, OP.add)
+
+    def select(k):
+        tr(R("xx" + k), R("xw" + k))
+        ts(R("cl" + k), R("xx" + k), c1(4), c1(5), OP.max, OP.min)
+        tt(R("s1" + k), R("cl" + k, ANY, S_(0, 16)), R("cl" + k, ANY, S_(16, 32)), OP.add)
+        tt(R("s2" + k), R("s1" + k, ANY, S_(0, 8)), R("s1" + k, ANY, S_(8, 16)), OP.add)
+        tt(R("s3" + k), R("s2" + k, ANY, S_(0, 4)), R("s2" + k, ANY, S_(4, 8)), OP.add)
+
+    def scores(r, x, a, n, q):
+        mm(x, cols("uc", 2 * x, 128), cols("upl", 2 * x, 128), *q_of(r, a, n), n)
+        frombank(q, cols("sct", NW * x + a, n), x, n)
+
+    def unpack(c, p, banks):
+        for b in range(4):
+            mm(banks + b, cols("ec", 128 * b, 128), cols("ep", 128 * b, 128), R(c), R(p))
+
+    for x in range(3):
+        scores(0, x, 0, C, "s")
+    for k in range(7):
+        rep(k)
+    for x in range(3, 8):
+        scores(0, x, 0, C, "s")
+    walk(0, dv_fill({(6, 0): [lambda: ts(R("d0"), cols("dd", 0, 8), float(NW), None, OP.mult)],
+                     (6, 1): [lambda: ts(R("dd2"), R("dd"), -2.0, None, OP.mult)],
+                     (3, 1): [lambda: ts(c1(5), c1(4), float(NW), None, OP.add)],
+                     (2, 1): [lambda: ts(c1(6), c1(3), 7.0 * NW, 7.0 * NW + 8 * BASE, OP.mult, OP.add)]}))
+    addresses()
+    list_of_addresses()
+    quant(R("ec"), R("ep"), R("ebt"))
+
+    for r in range(3):
+        odd = r == 1
+        gather("v", R("ev"), R("sct"), R("eb"))
+        unpack("qc%d" % r, "qp%d" % r, 0)
+        for b in range(4):
+            frombank("s", cols("fb", C * b, C), b)
+        n = 12 if odd else 16
+        if odd:
+            tt(cols("bt", 0, 192), cols("ev", 256, 192), cols("ev", 64, 192), OP.is_gt)
+        else:
+            tt(R("bt"), cols("ev", 0, 256), cols("ev", 256, 256), OP.is_gt)
+        for h in range(2):
+            ts(R("bd", S_(0, n), h, ANY), cols("bt", 0, 16 * n), c1(h), None, OP.mult)
+        tr(cols("btt", 0, 32 * n), R("bd", S_(0, n), ANY, ANY))
+        bm, bm0 = R("btt", S_(0, 32 * n, 16)), R("btt", S_(0, 128, 16))
+        m, m2 = cols("mm", 0, 2 * n), cols("mm2", 0, 2 * n)
+        mine = IO if odd else IE
+        first = 1 if odd else 0
+        tt(m2, bm, cols("dd2", 0, 2 * n), OP.mult)
+        tt(R("m0"), bm0, R("d0"), OP.mult)
+        tt(mine, mine, m2, OP.add)
+        tt(m, bm, cols("dd", 0, 2 * n), OP.mult)
+        if odd:
+            cp("v", cols("idxu", 32, 24), IO)
+            t0 = R("tt", S_(0, 128, 16))
+            tt(t0, t0, R("m0"), OP.add)
+            tt(cols("idxf", 0, 24), cols("idxf", 0, 24), m, OP.add)
+            cp("v", cols("offu", 8 * KAP[1], 8), t0)
+            tt(cols("idxf", 8, 24), cols("idxf", 8, 24), m, OP.add)
+        else:
+            cp("v", cols("idxu", 0, 32), IE)
+            tt(R("off0"), R("off0"), R("m0"), OP.add)
+            tt(IO, IO, cols("mm", 8, 24), OP.add)
+            cp("v", cols("offu", 0, 8), R("off0"))
+            tt(IO, IO, cols("mm", 0, 24), OP.add)
+        up, dn = (OP.subtract, OP.add) if odd else (OP.add, OP.subtract)
+        E, O = (cols("oe", 8, 24), cols("oo", 0, 24)) if odd else (oe, oo)
+        a, k = (0, 32) if odd else (32, 24)
+        rep(first)
+        cp("v", cols("idxu", a, k), cols("idxf", a, k))
+        for k in range(first + 1, 7):
+            rep(k)
+        walk(first, dv_fill({(3, 0): [lambda: tt(O, O, m, dn)], (3, 1): [lambda: tt(E, E, m, up)]}))
+        addresses()
+        tr(R("ltA"), R("vadr"))
+        list_of_addresses()
+        spread("ltA", "xdA", "xwA", 3)
+        gather("s", R("brep"), cols("tab", BASE, TW - BASE), R("eb"))
+        select("A")
+        ts(R("al%d" % r), R("s3A"), c1(6), None, OP.subtract)
+        remote(r, T["zl%d" % r][:], T["al%d" % r][:], "ra%d" % r, [R("al%d" % r)])
+        unpack("lc%d" % r, "lp%d" % r, 4)
+        for b in range(2):
+            frombank("s", cols("dp", C * b, C), 4 + b)
+        tr(R("brt"), R("brep"))
+        cp("v", R("lb"), R("brt", S_(0, 512, 16)))
+        tr(R("ltB"), R("lb"))
+        spread("ltB", "xdB", "xwB", 3)
+        for b in range(2, 4):
+            frombank("s", cols("dp", C * b, C), 4 + b)
+        select("B")
+        if r == 0:
+            quant(R("vq"), R("vp"), R("vb16"))
+        if r == 2:
+            tt(cols("olf", 0, 16), R("oe", S_(0, 32, 2)), R("oe", S_(1, 32, 2)), OP.add)
+            tt(cols("olf", 16, 16), R("oo", S_(0, 32, 2)), R("oo", S_(1, 32, 2)), OP.add)
+            ts(R("olg"), R("olf"), 4.0, -7.0, OP.is_ge, OP.mult)
+            tt(R("olf"), R("olf"), R("olf"), OP.add)
+            tt(R("olf"), R("olf"), R("olg"), OP.add)
+            tr(R("olt"), R("olf"))
+            items = []
+            for a in range(3):
+                for par in range(2):
+                    for h in range(2):
+                        p = slice(32 * a + 16 * par, 32 * a + 16 * par + 16)
+                        c = 128 * a + 64 * h
+                        items.append(("y", T.ol[par:8:2, c:c + 64], T.olt[p, 16 * h:16 * h + 16], [], [R("olt", S_(16 * h, 16 * h + 16), p=p)]))
+            dmas("d_ol", items)
+        zt, zl = "zt%d" % r, R("zl%d" % r)
+        for b in (0, 2, 1, 3):
+            gather("vs"[b // 2], R(zt, S_(b, 4 * C, 4)), cols("dp", C * b, C), zl)
+        quant(R("zc%d" % r), R("zp%d" % r), R(zt))
+        for l in range(2):
+            for h in range(2):
+                ts(R("b5", ANY, h, ANY, l), R("s3B", S_(l, 6, 2), S_(h, 4, 2)), c1(6), None, OP.subtract)
+        cp("v", R("bl"), R("b5"))
+        if r < 2:
+            w = 24 if r == 0 else 32
+            tt(cols("dd", 0, w), IO if r == 0 else IE, cols("mk8", 0, w), OP.subtract)
+            ts(cols("dd2", 0, w), cols("dd", 0, w), -2.0, None, OP.mult)
+            ts(R("d0"), cols("dd", 0, 8), float(NW), None, OP.mult)
+        nx = "xs%d" % (r + 1)
+        for b in range(4):
+            mm(b, cols("wcod", 128 * b, 128), cols("wpl", 128 * b, 128), R("zc%d" % r), R("zp%d" % r))
+            frombank("s", cols("rs", C * b, C), b, C, 0.03125)
+        hc = C // 2
+        for h in range(2):
+            for b in range(4):
+                gather_add(R(nx, S_(4 * hc * h + b, 4 * hc * (h + 1), 4)), cols("rs", C * b, C), cols("bl", 12 * h, 12), cols("fb", C * b + hc * h, hc))
+            quant(*q_of(r + 1, hc * h, hc), cols(nx, 4 * hc * h, 4 * hc))
+            if r < 2:
+                for x in range(8):
+                    scores(r + 1, x, hc * h, hc, "s" if h == 0 else "vs"[x % 2])
+        if r < 2:
+            send_state(r + 1)
+
+    qc, qp = q_of(3)
+    mm(0, R("vq"), R("vp"), qc, qp)
+    dmas("d_o", [("y", T.oc[:], T.qc3[:].bitcast(dt.uint8), [], [qc])]
+         + [(("s", "y")[k % 2], T.osc[4 * k:4 * k + 4, :], T.qp3[32 * k:32 * k + 4, :], [], [qp]) for k in range(4)])
+    frombank("v", R("ys"), 0)
+    dmas("d_y", [("y", T.y[:], T.ys[:], [], [R("ys")])])
+    finish()

@@ -2,6 +2,7 @@ import numpy as np
 from concourse.mybir import dt, AluOpType, ActivationFunctionType
 
 C = 384
+HC = C // 2
 STEP = [2, 3, 1]
 NW = 512
 BASE = 8
@@ -9,6 +10,10 @@ TW = BASE + 8 * NW
 OP = AluOpType
 COPY = ActivationFunctionType.Copy
 F32, BF, I32, U16, X4, U8 = "float32", "bfloat16", "int32", "uint16", "float8_e4m3fn_x4", "uint8"
+SMALL = {}
+for _n, _w in (("js", 4), ("jbm", 8), ("dd", 32), ("dd2", 32), ("d0", 8), ("mm", 32), ("mm2", 32), ("m0", 8), ("dv", 32), ("off0", 8), ("offsf", 8),
+               ("idxs", 8), ("y0", 8), ("y1", 8), ("yt", 8), ("yk", 8), ("t1", 8), ("t2", 8), ("t3", 8)):
+    SMALL[_n] = (sum(k[1] for k in SMALL.values()), _w)
 
 
 def _scratch():
@@ -19,7 +24,7 @@ def _scratch():
     sb("pgi", [24], I32); sb("ogi", [24], I32); sb("pidx", [1], I32); sb("ti", [8], I32); sb("t24", [24], I32); sb("t24b", [24], I32)
     sb("selu", [10], U16); sb("win", [16], F32); sb("wini", [16], I32)
     sb("pgf", [32], F32); sb("pgt", [32], F32); sb("ogf", [32], F32); sb("ogt", [32], F32)
-    sb("cst", [16], F32); sb("one16", [16], F32); sb("js", [4], F32); sb("mk8", [32], F32); sb("jbm", [8], F32)
+    sb("cst", [16], F32); sb("one16", [16], F32); sb("mk8", [32], F32); sb("sm", [sum(k[1] for k in SMALL.values())], F32)
     sb("ones", [512], BF); sb("ebt", [2048], BF); sb("ec", [512], X4); sb("ep", [512], U8)
     sb("xb", [4 * C], BF); sb("ub", [512], BF); sb("vb16", [512], BF)
     sb("uq0", [128], X4); sb("up0", [128], U8); sb("uc", [160], X4); sb("upl", [160], U8)
@@ -32,26 +37,25 @@ def _scratch():
     for r in range(3):
         sb("lc%d" % r, [C], X4); sb("lp%d" % r, [C], U8); sb("zl%d" % r, [24], U16); sb("al%d" % r, [24], U16)
         sb("zc%d" % r, [C], X4); sb("zp%d" % r, [C], U8); sb("zt%d" % r, [4 * C], BF)
-    sb("fb", [4 * C], BF); sb("dp", [4 * C], BF); sb("rs", [4 * C], F32)
+    sb("fb", [3 * C], BF); sb("dp", [4 * C], BF); sb("rs", [4 * C], F32); sb("gs", [C], F32)
     sb("oxd", [64], F32); sb("oxw", [256], F32); sb("ox", [4, 2, 32], F32)
-    sb("oe", [32], F32); sb("oo", [32], F32)
-    sb("dd", [32], F32); sb("dd2", [32], F32); sb("d0", [8], F32); sb("mm", [32], F32); sb("mm2", [32], F32); sb("m0", [8], F32)
-    sb("idxf", [64], F32); sb("idxu", [64], U16); sb("dv", [32], F32); sb("off0", [8], F32)
+    sb("oe", [32], F32); sb("oo", [32], F32); sb("idxf", [64], F32); sb("idxu", [64], U16); sb("idxsu", [8], U16)
     sb("offu", [64], U16); sb("wk", [1024], F32); sb("tt", [1024], F32); sb("rep", [1024], F32)
     sb("vs", [32], F32); sb("vadr", [32], F32); sb("eb", [32], U16)
     sb("ev", [512], F32); sb("bt", [256], BF); sb("bd", [16, 2, 16], BF); sb("btt", [512], BF)
     sb("brep", [512], F32); sb("brt", [512], F32); sb("lb", [32], F32)
+    sb("zm", [192], F32); sb("offs", [16], U16); sb("reps", [128], F32); sb("wks", [256], F32); sb("tts", [256], F32)
     for k in ("A", "B"):
         sb("lt" + k, [32], F32); sb("xd" + k, [64], F32); sb("xw" + k, [192], F32); sb("xx" + k, [192], F32)
-        sb("cl" + k, [6, 32], F32); sb("s1" + k, [6, 16], F32); sb("s2" + k, [6, 8], F32); sb("s3" + k, [6, 4], F32)
-    sb("b5", [3, 2, 2, 2], F32); sb("bl", [24], U16)
+        sb("cl" + k, [192], F32); sb("sc" + k, [192], F32)
+    sb("bl", [24], U16)
     sb("olf", [32], F32); sb("olg", [32], F32); sb("olt", [32], F32); sb("ys", [C], F32)
     s["ps"] = ("psum", [128, 4096], F32)
     return s
 
 
 SCRATCH = _scratch()
-SEMAPHORES = (["qv", "qs", "qt", "qg", "loc", "d_pg", "d_og", "d_x", "d_u", "d_w", "d_v", "d_t", "d_o", "d_ol", "d_y"]
+SEMAPHORES = (["qv", "qs", "qt", "qg", "loc", "d_pg", "d_og", "d_x", "d_u", "d_w", "d_v", "d_t", "d_o", "d_ol", "d_y0", "d_y1"]
               + ["rq%d" % r for r in range(3)] + ["ra%d" % r for r in range(3)])
 
 
@@ -102,7 +106,7 @@ def make_queue_tools(g, T):
             for ref in refs:
                 p0, p1, m = region(ref)
                 for (h0, h1, hm, hw, hq, he) in hist.get(ref[0], ()):
-                    if (hw or write) and h0 < p1 and p0 < h1 and hm & m:
+                    if (hw or write or ref[0] == "ps" and hq != q) and h0 < p1 and p0 < h1 and hm & m:
                         if not hw and hq == q:
                             continue
                         ev.append(he)
@@ -168,6 +172,10 @@ def rank_program(g, core, T, topo):
     ANY = slice(None)
 
     def R(name, *idx, p=slice(0, 128)):
+        if name in SMALL:
+            o, n = SMALL[name]
+            i = idx[0] if idx else slice(0, n)
+            name, idx = "sm", (slice(o + i.start, o + i.stop, i.step),)
         return (name, (p,) + tuple(idx)) if idx else (name, (p,) + tuple(ANY for _ in SCRATCH[name][1][1:]))
 
     def V(ref):
@@ -303,11 +311,21 @@ def rank_program(g, core, T, topo):
 
     ts(R("t24"), R("ogi"), 1, None, OP.bitwise_and)
     ts(R("t24b"), R("ogi"), 1, None, OP.arith_shift_right)
+    cp("v", c1(1), ti(0))
+    ts(c1(0), ti(0), -1.0, 1.0, OP.mult, OP.add)
     ts(R("t24"), R("t24"), 4.0, None, OP.mult)
     ms(R("one16"), 1.0)
+    ts(c1(7), ti(1), 128.0, None, OP.mult)
+    ts(c1(8), ti(0), 64.0, None, OP.mult)
     tt(cols("ogf", 0, 24), R("t24"), R("t24b"), OP.add)
     ts(ti(3), R("pidx"), 1, 3, OP.arith_shift_right, OP.bitwise_and)
+    cp("v", R("win"), R("wini"))
+    tt(c1(7), c1(7), c1(8), OP.add)
     tr(R("ogt"), R("ogf"))
+    for h in range(2):
+        ts(R("mk8", S_(h, 32, 2)), R("one16"), c1(h), 8.0, OP.mult, OP.mult)
+    tt(c1(7), c1(7), ti(2), OP.add)
+    ms(cols("win", 0, 1), 0.0)
 
     def spread(src, xd, xw, nsrc):
         for H in range(2):
@@ -320,22 +338,17 @@ def rank_program(g, core, T, topo):
                 k += 1
 
     spread("ogt", "oxd", "oxw", 4)
-    quant(*q_of(0), R("xb"))
-    send_state(0)
-    for x in range(8):
-        iota(cols("sct", NW * x + C, NW - C), [[0, NW - C]], 0, 0, allow_small_or_imprecise_dtypes=True)
+    for s in range(4):
+        ts(cols("js", s, 1), c1(7), 16.0 * s + BASE, None, OP.add)
+    cp("v", cols("idxf", 56, 8), cols("mk8", 0, 8))
+    for h in range(2):
+        ts(R("jbm", S_(h, 8, 2)), R("js"), c1(h), None, OP.mult)
     ts(ti(4), R("pidx"), 3, 1, OP.arith_shift_right, OP.bitwise_and)
-    cp("v", c1(1), ti(0))
     ts(c1(9), ti(3), 32.0, None, OP.mult)
     ts(c1(10), ti(4), 16.0, None, OP.mult)
     tr(R("ox"), R("oxw"))
     tt(c1(9), c1(9), c1(10), OP.add)
-    ts(c1(0), ti(0), -1.0, 1.0, OP.mult, OP.add)
     ts(R("selu"), cols("one16", 0, 10), c1(9), None, OP.mult)
-    quant(R("uq0"), R("up0"), R("ub"))
-    op("v", lambda: g.vector.tensor_copy(T.uc[:].bitcast(dt.uint32), T.uq0[:].bitcast(dt.uint32).indirect(T.selu[:])),
-       [R("uc")], [R("uq0"), R("selu")])
-    op("s", lambda: g.scalar.activation(T.upl[:], T.up0[:].indirect(T.selu[:]), COPY), [R("upl")], [R("up0"), R("selu")])
     for par, name in ((0, "oe"), (1, "oo")):
         for a in range(4):
             for h in range(2):
@@ -348,25 +361,12 @@ def rank_program(g, core, T, topo):
                     ts(o, i, s, None, OP.mult)
     oe, oo, mk8 = R("oe"), R("oo"), R("mk8")
     IE, IO = cols("idxf", 0, 32), cols("idxf", 32, 24)
-    for h in range(2):
-        ts(R("mk8", S_(h, 32, 2)), R("one16"), c1(h), 8.0, OP.mult, OP.mult)
-    ts(c1(7), ti(1), 128.0, None, OP.mult)
-    ts(c1(8), ti(0), 64.0, None, OP.mult)
-    cp("v", R("win"), R("wini"))
-    tt(c1(7), c1(7), c1(8), OP.add)
-    cp("v", cols("idxf", 56, 8), cols("mk8", 0, 8))
-    tt(c1(7), c1(7), ti(2), OP.add)
-    ms(cols("win", 0, 1), 0.0)
     tt(R("dd"), oo, oe, OP.subtract)
     tt(IO, cols("oe", 8, 24), cols("oo", 0, 24), OP.subtract)
     tt(IE, R("dd"), mk8, OP.add)
     tt(IO, IO, cols("mk8", 0, 24), OP.add)
-    for s in range(4):
-        ts(cols("js", s, 1), c1(7), 16.0 * s + BASE, None, OP.add)
     cp("v", R("idxu"), R("idxf"))
     ts(R("off0"), cols("oe", 0, 8), float(NW), None, OP.mult)
-    for h in range(2):
-        ts(R("jbm", S_(h, 8, 2)), R("js"), c1(h), None, OP.mult)
     tt(R("off0"), R("off0"), R("jbm"), OP.add)
     cp("v", cols("offu", 0, 8), R("off0"))
 
@@ -381,62 +381,122 @@ def rank_program(g, core, T, topo):
             blk, off = (128 * z, 128), cols("offu", 8 * z, 8)
             if k < 7:
                 gather_add(cols("wk", *blk), R("tab"), off, cols("rep", *blk))
+                pause(fill)
             else:
                 gather("v", cols("wk", *blk), R("tab"), off)
-            for f in fill.pop((k, 0), ()):
-                f()
+                early_addresses(2)
             tr(cols("tt", *blk), cols("wk", *blk))
-            for f in fill.pop((k, 1), ()):
-                f()
+            if k < 6:
+                pause(fill)
+            elif k == 6:
+                early_addresses(0)
             if k < 7:
                 cp("v", cols("offu", 8 * KAP[k + 1], 8), R("tt", S_(128 * z, 128 * z + 128, 16)))
+                if k == 6:
+                    early_addresses(1)
+                else:
+                    pause(fill)
 
-    def dv_fill(fill):
-        fill.setdefault((4, 1), []).append(lambda: tt(R("dv"), R("idxf", S_(0, 64, 2)), R("idxf", S_(1, 64, 2)), OP.add))
-        fill.setdefault((5, 1), []).append(lambda: ts(R("dv"), R("dv"), -float(NW), 8.0 * NW, OP.mult, OP.add))
-        return fill
+    def pause(fill):
+        if fill:
+            fill.pop(0)()
 
-    def addresses():
-        tt(R("vs"), R("tt", S_(0, 1024, 32)), R("tt", S_(16, 1024, 32)), OP.add)
-        tt(R("vadr"), R("vs"), R("dv"), OP.add)
+    def differences():
+        return [lambda: tt(R("dv"), R("idxf", S_(0, 64, 2)), R("idxf", S_(1, 64, 2)), OP.add),
+                lambda: ts(R("dv"), R("dv"), -float(NW), 8.0 * NW, OP.mult, OP.add)]
+
+    def early_addresses(step):
+        if step == 0:
+            tt(cols("vs", 0, 28), R("tt", S_(0, 896, 32)), R("tt", S_(16, 896, 32)), OP.add)
+        elif step == 1:
+            tt(cols("vs", 0, 28), cols("vs", 0, 28), cols("dv", 0, 28), OP.add)
+        else:
+            for s in range(4):
+                cp("v", R("vadr", S_(8 * s, 8 * s + 7)), R("vs", S_(s, 28, 4)))
+
+    def last_address():
+        tt(R("vadr", S_(7, 32, 8)), R("tt", S_(896, 1024, 32)), R("tt", S_(912, 1024, 32)), OP.add)
 
     def list_of_addresses():
-        ts(R("eb"), R("vadr"), -float(BASE), None, OP.add)
+        ts(cols("eb", 0, 28), cols("vs", 0, 28), -float(BASE), None, OP.add)
+        ts(cols("eb", 28, 4), R("vadr", S_(7, 32, 8)), -float(BASE), None, OP.add)
+
+    def tt8(k):
+        return R("tt", S_(128 * KAP[k], 128 * KAP[k] + 128, 16))
+
+    def ahead(k, even):
+        w = 32 if even else 24
+        src = IE if even else IO
+        s0, s1 = R("tts", S_(0, 128, 16)), R("tts", S_(128, 256, 16))
+        nxt = cols("idxf", 8 * KAP[k + 1], 8)
+        return [
+            lambda: tt(cols("dd", 0, w), src, cols("mk8", 0, w), OP.subtract),
+            lambda: (ts(R("d0"), cols("dd", 0, 8), float(NW), None, OP.mult), tt(R("idxs"), cols("mk8", 0, 8), cols("dd", 0, 8), OP.subtract)),
+            lambda: (tt(R("offsf"), R("off0") if even else tt8(0), R("d0"), OP.add), cp("v", R("idxsu"), R("idxs"))),
+            lambda: (cp("v", cols("offs", 0, 8), R("offsf")), gather("s", R("reps"), R("win"), R("idxsu"))),
+            lambda: gather_add(cols("wks", 0, 128), R("tab"), cols("offs", 0, 8), R("reps")),
+            lambda: tr(cols("tts", 0, 128), cols("wks", 0, 128)),
+            lambda: cp("v", cols("offs", 8, 8), s0),
+            lambda: gather("v", cols("wks", 128, 128), R("tab"), cols("offs", 8, 8)),
+            lambda: tr(cols("tts", 128, 128), cols("wks", 128, 128)),
+            lambda: (tt(R("yk"), nxt, cols("mk8", 0, 8), OP.subtract), tt(R("yt"), s1, tt8(k + 1), OP.subtract),
+                     ts(cols("dd2", 0, w), cols("dd", 0, w), -2.0, None, OP.mult)),
+            lambda: (tt(R("yk"), R("yk"), cols("dd", 0, 8), OP.add), tt(R("y0"), s0, tt8(k), OP.subtract)),
+            lambda: (ts(R("yk"), R("yk"), float(NW), None, OP.mult), ts(R("t3"), cols("dd", 8, 8), float(NW), None, OP.mult)),
+            lambda: tt(R("y1"), R("yt"), R("yk"), OP.add),
+        ]
 
     def select(k):
         tr(R("xx" + k), R("xw" + k))
         ts(R("cl" + k), R("xx" + k), c1(4), c1(5), OP.max, OP.min)
-        tt(R("s1" + k), R("cl" + k, ANY, S_(0, 16)), R("cl" + k, ANY, S_(16, 32)), OP.add)
-        tt(R("s2" + k), R("s1" + k, ANY, S_(0, 8)), R("s1" + k, ANY, S_(8, 16)), OP.add)
-        tt(R("s3" + k), R("s2" + k, ANY, S_(0, 4)), R("s2" + k, ANY, S_(4, 8)), OP.add)
 
-    def scores(r, x, a, n, q):
-        mm(x, cols("uc", 2 * x, 128), cols("upl", 2 * x, 128), *q_of(r, a, n), n)
-        frombank(q, cols("sct", NW * x + a, n), x, n)
+    def totals(k):
+        op("v", lambda: g.vector.tensor_tensor_scan(V(R("sc" + k)), V(R("zm")), V(R("cl" + k)), 0.0, OP.mult, OP.add),
+           [R("sc" + k)], [R("zm"), R("cl" + k)])
+
+    def scores(r, x, a, n, q, k):
+        mm(k, cols("uc", 2 * x, 128), cols("upl", 2 * x, 128), *q_of(r, a, n), n)
+        frombank(q, cols("sct", NW * x + a, n), k, n)
 
     def unpack(c, p, banks):
         for b in range(4):
             mm(banks + b, cols("ec", 128 * b, 128), cols("ep", 128 * b, 128), R(c), R(p))
 
-    for x in range(3):
-        scores(0, x, 0, C, "s")
     for k in range(7):
         rep(k)
-    for x in range(3, 8):
-        scores(0, x, 0, C, "s")
-    walk(0, dv_fill({(6, 0): [lambda: ts(R("d0"), cols("dd", 0, 8), float(NW), None, OP.mult)],
-                     (6, 1): [lambda: ts(R("dd2"), R("dd"), -2.0, None, OP.mult)],
-                     (3, 1): [lambda: ts(c1(5), c1(4), float(NW), None, OP.add)],
-                     (2, 1): [lambda: ts(c1(6), c1(3), 7.0 * NW, 7.0 * NW + 8 * BASE, OP.mult, OP.add)]}))
-    addresses()
+
+    def first_state():
+        quant(*q_of(0), R("xb"))
+        send_state(0)
+        for x in range(8):
+            iota(cols("sct", NW * x + C, NW - C), [[0, NW - C]], 0, 0, allow_small_or_imprecise_dtypes=True)
+
+    def scoring_columns():
+        op("v", lambda: g.vector.tensor_copy(T.uc[:].bitcast(dt.uint32), T.uq0[:].bitcast(dt.uint32).indirect(T.selu[:])),
+           [R("uc")], [R("uq0"), R("selu")])
+        op("s", lambda: g.scalar.activation(T.upl[:], T.up0[:].indirect(T.selu[:]), COPY), [R("upl")], [R("up0"), R("selu")])
+    aim = ahead(0, True)
+    fill = aim[:4] + [lambda: quant(R("uq0"), R("up0"), R("ub")), first_state, scoring_columns] + differences() + aim[4:] + [
+        lambda: ms(R("zm"), 1.0),
+        lambda: ms(R("zm", S_(0, 192, 8)), 0.0),
+        lambda: ts(c1(5), c1(4), float(NW), None, OP.add),
+        lambda: ts(c1(6), c1(3), 7.0 * NW, 7.0 * NW + 8 * BASE, OP.mult, OP.add)]
+    walk(0, fill)
+    for x in range(8):
+        scores(0, x, 0, C, "s", x)
+    last_address()
     list_of_addresses()
-    quant(R("ec"), R("ep"), R("ebt"))
 
     for r in range(3):
         odd = r == 1
-        gather("v", R("ev"), R("sct"), R("eb"))
+        for k in range(2):
+            gather("vs"[k], cols("ev", 256 * k, 256), R("sct"), cols("eb", 16 * k, 16))
+        while fill:
+            pause(fill)
+        if r == 0:
+            quant(R("ec"), R("ep"), R("ebt"))
         unpack("qc%d" % r, "qp%d" % r, 0)
-        for b in range(4):
+        for b in range(3):
             frombank("s", cols("fb", C * b, C), b)
         n = 12 if odd else 16
         if odd:
@@ -446,55 +506,68 @@ def rank_program(g, core, T, topo):
         for h in range(2):
             ts(R("bd", S_(0, n), h, ANY), cols("bt", 0, 16 * n), c1(h), None, OP.mult)
         tr(cols("btt", 0, 32 * n), R("bd", S_(0, n), ANY, ANY))
-        bm, bm0 = R("btt", S_(0, 32 * n, 16)), R("btt", S_(0, 128, 16))
+        bm, bm0, bm1 = R("btt", S_(0, 32 * n, 16)), R("btt", S_(0, 128, 16)), R("btt", S_(128, 256, 16))
         m, m2 = cols("mm", 0, 2 * n), cols("mm2", 0, 2 * n)
         mine = IO if odd else IE
         first = 1 if odd else 0
+        t0, t1, t2 = tt8(0), tt8(first), tt8(first + 1)
         tt(m2, bm, cols("dd2", 0, 2 * n), OP.mult)
-        tt(R("m0"), bm0, R("d0"), OP.mult)
+        tt(R("t1"), bm0, R("y1"), OP.mult)
+        tt(R("t2"), bm1, R("t3"), OP.mult)
         tt(mine, mine, m2, OP.add)
+        tt(t2, t2, R("t1"), OP.add)
         tt(m, bm, cols("dd", 0, 2 * n), OP.mult)
         if odd:
             cp("v", cols("idxu", 32, 24), IO)
-            t0 = R("tt", S_(0, 128, 16))
-            tt(t0, t0, R("m0"), OP.add)
-            tt(cols("idxf", 0, 24), cols("idxf", 0, 24), m, OP.add)
-            cp("v", cols("offu", 8 * KAP[1], 8), t0)
-            tt(cols("idxf", 8, 24), cols("idxf", 8, 24), m, OP.add)
         else:
             cp("v", cols("idxu", 0, 32), IE)
-            tt(R("off0"), R("off0"), R("m0"), OP.add)
+        tt(t2, t2, R("t2"), OP.add)
+        rep(first + 2)
+        a, k = (0, 32) if odd else (32, 24)
+        if odd:
+            tt(cols("idxf", 0, 24), cols("idxf", 0, 24), m, OP.add)
+        else:
             tt(IO, IO, cols("mm", 8, 24), OP.add)
-            cp("v", cols("offu", 0, 8), R("off0"))
+        cp("v", cols("offu", 8 * KAP[first + 2], 8), t2)
+        if odd:
+            tt(cols("idxf", 8, 24), cols("idxf", 8, 24), m, OP.add)
+        else:
             tt(IO, IO, cols("mm", 0, 24), OP.add)
+        tt(R("m0"), bm0, R("d0"), OP.mult)
+        cp("v", cols("idxu", a, k), cols("idxf", a, k))
+        for k in range(first + 3, 7):
+            rep(k)
         up, dn = (OP.subtract, OP.add) if odd else (OP.add, OP.subtract)
         E, O = (cols("oe", 8, 24), cols("oo", 0, 24)) if odd else (oe, oo)
-        a, k = (0, 32) if odd else (32, 24)
-        rep(first)
-        cp("v", cols("idxu", a, k), cols("idxf", a, k))
-        for k in range(first + 1, 7):
-            rep(k)
-        walk(first, dv_fill({(3, 0): [lambda: tt(O, O, m, dn)], (3, 1): [lambda: tt(E, E, m, up)]}))
-        addresses()
+        f0 = t0 if odd else R("off0")
+        diff = differences()
+        fill = [lambda: (tt(R("y0"), bm0, R("y0"), OP.mult), tt(f0, f0, R("m0"), OP.add)), lambda: (tt(t1, t1, R("y0"), OP.add), diff[0]())]
+        fill += ahead(0 if odd else 1, odd) if r < 2 else []
+        orders = lambda: (tt(O, O, m, dn), tt(E, E, m, up))
+        fill.insert(3, lambda: (diff[1](), orders()))
+        if r == 0:
+            fill.append(lambda: quant(R("vq"), R("vp"), R("vb16")))
+        walk(first + 2, fill)
+        last_address()
         tr(R("ltA"), R("vadr"))
         list_of_addresses()
         spread("ltA", "xdA", "xwA", 3)
         gather("s", R("brep"), cols("tab", BASE, TW - BASE), R("eb"))
         select("A")
-        ts(R("al%d" % r), R("s3A"), c1(6), None, OP.subtract)
+        totals("A")
+        ts(R("al%d" % r), R("scA", S_(7, 192, 8)), c1(6), None, OP.subtract)
         remote(r, T["zl%d" % r][:], T["al%d" % r][:], "ra%d" % r, [R("al%d" % r)])
         unpack("lc%d" % r, "lp%d" % r, 4)
         for b in range(2):
             frombank("s", cols("dp", C * b, C), 4 + b)
         tr(R("brt"), R("brep"))
-        cp("v", R("lb"), R("brt", S_(0, 512, 16)))
+        for k in range(4):
+            cp("v", cols("lb", 8 * k, 8), R("brt", S_(16 * k, 512, 64)))
         tr(R("ltB"), R("lb"))
         spread("ltB", "xdB", "xwB", 3)
         for b in range(2, 4):
             frombank("s", cols("dp", C * b, C), 4 + b)
         select("B")
-        if r == 0:
-            quant(R("vq"), R("vp"), R("vb16"))
         if r == 2:
             tt(cols("olf", 0, 16), R("oe", S_(0, 32, 2)), R("oe", S_(1, 32, 2)), OP.add)
             tt(cols("olf", 16, 16), R("oo", S_(0, 32, 2)), R("oo", S_(1, 32, 2)), OP.add)
@@ -510,38 +583,48 @@ def rank_program(g, core, T, topo):
                         c = 128 * a + 64 * h
                         items.append(("y", T.ol[par:8:2, c:c + 64], T.olt[p, 16 * h:16 * h + 16], [], [R("olt", S_(16 * h, 16 * h + 16), p=p)]))
             dmas("d_ol", items)
-        zt, zl = "zt%d" % r, R("zl%d" % r)
-        for b in (0, 2, 1, 3):
-            gather("vs"[b // 2], R(zt, S_(b, 4 * C, 4)), cols("dp", C * b, C), zl)
-        quant(R("zc%d" % r), R("zp%d" % r), R(zt))
-        for l in range(2):
-            for h in range(2):
-                ts(R("b5", ANY, h, ANY, l), R("s3B", S_(l, 6, 2), S_(h, 4, 2)), c1(6), None, OP.subtract)
-        cp("v", R("bl"), R("b5"))
-        if r < 2:
-            w = 24 if r == 0 else 32
-            tt(cols("dd", 0, w), IO if r == 0 else IE, cols("mk8", 0, w), OP.subtract)
-            ts(cols("dd2", 0, w), cols("dd", 0, w), -2.0, None, OP.mult)
-            ts(R("d0"), cols("dd", 0, 8), float(NW), None, OP.mult)
-        nx = "xs%d" % (r + 1)
-        for b in range(4):
-            mm(b, cols("wcod", 128 * b, 128), cols("wpl", 128 * b, 128), R("zc%d" % r), R("zp%d" % r))
-            frombank("s", cols("rs", C * b, C), b, C, 0.03125)
-        hc = C // 2
+        zt, zc, zp = "zt%d" % r, "zc%d" % r, "zp%d" % r
         for h in range(2):
-            for b in range(4):
-                gather_add(R(nx, S_(4 * hc * h + b, 4 * hc * (h + 1), 4)), cols("rs", C * b, C), cols("bl", 12 * h, 12), cols("fb", C * b + hc * h, hc))
-            quant(*q_of(r + 1, hc * h, hc), cols(nx, 4 * hc * h, 4 * hc))
+            for b in (0, 2, 1, 3):
+                gather("vs"[b // 2], R(zt, S_(4 * HC * h + b, 4 * HC * (h + 1), 4)), cols("dp", C * b, C), cols("zl%d" % r, 12 * h, 12))
+        totals("B")
+        for h in range(2):
+            quant(cols(zc, HC * h, HC), cols(zp, HC * h, HC), cols(zt, 4 * HC * h, 4 * HC))
+        for k in range(4):
+            for l in range(2):
+                ts(R("bl", S_(4 * (k & 1) + (k & 2) + l, 24, 8)), R("scB", S_(32 * l + 8 * k + 7, 192, 64)), c1(6), None, OP.subtract)
+        for h in range(2):
+            mm(h, cols("wcod", 0, 128), cols("wpl", 0, 128), cols(zc, HC * h, HC), cols(zp, HC * h, HC), HC)
+            frombank("sv"[h], cols("rs", HC * h, HC), h, HC, 0.03125)
+        nx = "xs%d" % (r + 1)
+        for b, k in ((1, 2), (3, 5), (2, 4)):
+            mm(k, cols("wcod", 128 * b, 128), cols("wpl", 128 * b, 128), R(zc), R(zp))
+            frombank("s", cols("rs", C * b, C), k, C, 0.03125)
+        for h in range(2):
+            gather("s", cols("gs", HC * h, HC), cols("rs", 3 * C, C), cols("bl", 12 * h, 12))
+        for h in range(2):
+            for b in range(3):
+                gather_add(R(nx, S_(4 * HC * h + b, 4 * HC * (h + 1), 4)), cols("rs", C * b, C), cols("bl", 12 * h, 12), cols("fb", C * b + HC * h, HC))
+            o, i = R(nx, S_(4 * HC * h + 3, 4 * HC * (h + 1), 4)), cols("gs", HC * h, HC)
+            op("v", lambda: g.vector.tensor_tensor(V(o), V(i), T.ps[:, 512 * 3 + HC * h:512 * 3 + HC * h + HC], OP.add), [o], [i, ("ps", 3)])
+            quant(*q_of(r + 1, HC * h, HC), cols(nx, 4 * HC * h, 4 * HC))
             if r < 2:
                 for x in range(8):
-                    scores(r + 1, x, hc * h, hc, "s" if h == 0 else "vs"[x % 2])
+                    if h == 0:
+                        scores(r + 1, x, 0, HC, "s", (0, 1, 2, 6, 7, 5, 4, 0)[x])
+                    else:
+                        scores(r + 1, x, HC, HC, "sv"[x % 2], x)
+                        pause(fill)
+            else:
+                mm(h, R("vq"), R("vp"), *q_of(3, HC * h, HC), HC)
+                frombank("sv"[h], cols("ys", HC * h, HC), h, HC)
+                dmas("d_y%d" % h, [("y", T.y[:, HC * h:HC * h + HC], T.ys[:, HC * h:HC * h + HC], [], [cols("ys", HC * h, HC)])])
+        while fill:
+            pause(fill)
         if r < 2:
             send_state(r + 1)
 
     qc, qp = q_of(3)
-    mm(0, R("vq"), R("vp"), qc, qp)
-    dmas("d_o", [("y", T.oc[:], T.qc3[:].bitcast(dt.uint8), [], [qc])]
+    dmas("d_o", [("s", T.oc[:], T.qc3[:].bitcast(dt.uint8), [], [qc])]
          + [(("s", "y")[k % 2], T.osc[4 * k:4 * k + 4, :], T.qp3[32 * k:32 * k + 4, :], [], [qp]) for k in range(4)])
-    frombank("v", R("ys"), 0)
-    dmas("d_y", [("y", T.y[:], T.ys[:], [], [R("ys")])])
     finish()

import numpy as np
from concourse.mybir import dt, AluOpType, ActivationFunctionType

C = 384
HC = C // 2
STEP = [2, 3, 1]
NW = 512
BASE = 8
TW = BASE + 8 * NW
OP = AluOpType
COPY = ActivationFunctionType.Copy
F32, BF, I32, U16, X4, U8 = "float32", "bfloat16", "int32", "uint16", "float8_e4m3fn_x4", "uint8"
SMALL = {}
for _n, _w in (("js", 4), ("jbm", 8), ("dd", 32), ("dd2", 32), ("d0", 8), ("mm", 32), ("mm2", 32), ("m0", 8), ("dv", 32), ("off0", 8), ("offsf", 8),
               ("idxs", 8), ("y0", 8), ("y1", 8), ("yt", 8), ("yk", 8), ("t1", 8), ("t2", 8), ("t3", 8)):
    SMALL[_n] = (sum(k[1] for k in SMALL.values()), _w)


def _scratch():
    s = {}

    def sb(name, shape, d):
        s[name] = ("sbuf", [128] + shape, d)
    sb("pgi", [24], I32); sb("ogi", [24], I32); sb("pidx", [1], I32); sb("ti", [8], I32); sb("t24", [24], I32); sb("t24b", [24], I32)
    sb("selu", [10], U16); sb("win", [16], F32); sb("wini", [16], I32)
    sb("pgf", [32], F32); sb("pgt", [32], F32); sb("ogf", [32], F32); sb("ogt", [32], F32)
    sb("cst", [16], F32); sb("one16", [16], F32); sb("mk8", [32], F32); sb("sm", [sum(k[1] for k in SMALL.values())], F32)
    sb("ones", [512], BF); sb("ebt", [2048], BF); sb("ec", [512], X4); sb("ep", [512], U8)
    sb("xb", [4 * C], BF); sb("ub", [512], BF); sb("vb16", [512], BF)
    sb("uq0", [128], X4); sb("up0", [128], U8); sb("uc", [160], X4); sb("upl", [160], U8)
    sb("vq", [128], X4); sb("vp", [128], U8); sb("wcod", [512], X4); sb("wpl", [512], U8)
    sb("tab", [TW], F32); sb("sct", [8 * NW], F32)
    for r in range(4):
        sb("qc%d" % r, [C], X4); sb("qp%d" % r, [C], U8)
        if r:
            sb("xs%d" % r, [4 * C], BF)
    for r in range(3):
        sb("lc%d" % r, [C], X4); sb("lp%d" % r, [C], U8); sb("zl%d" % r, [24], U16); sb("al%d" % r, [24], U16)
        sb("zc%d" % r, [C], X4); sb("zp%d" % r, [C], U8); sb("zt%d" % r, [4 * C], BF)
    sb("fb", [3 * C], BF); sb("dp", [4 * C], BF); sb("rs", [4 * C], F32); sb("gs", [C], F32)
    sb("oxd", [64], F32); sb("oxw", [256], F32); sb("ox", [4, 2, 32], F32)
    sb("oe", [32], F32); sb("oo", [32], F32); sb("idxf", [64], F32); sb("idxu", [64], U16); sb("idxsu", [8], U16)
    sb("offu", [64], U16); sb("wk", [1024], F32); sb("tt", [1024], F32); sb("rep", [1024], F32)
    sb("vs", [32], F32); sb("vadr", [32], F32); sb("eb", [32], U16)
    sb("ev", [512], F32); sb("bt", [256], BF); sb("bd", [16, 2, 16], BF); sb("btt", [512], BF)
    sb("brep", [512], F32); sb("brt", [512], F32); sb("lb", [32], F32)
    sb("zm", [192], F32); sb("offs", [16], U16); sb("reps", [128], F32); sb("wks", [256], F32); sb("tts", [256], F32)
    for k in ("A", "B"):
        sb("lt" + k, [32], F32); sb("xd" + k, [64], F32); sb("xw" + k, [192], F32); sb("xx" + k, [192], F32)
        sb("cl" + k, [192], F32); sb("sc" + k, [192], F32)
    sb("bl", [24], U16)
    sb("olf", [32], F32); sb("olg", [32], F32); sb("olt", [32], F32); sb("ys", [C], F32)
    s["ps"] = ("psum", [128, 4096], F32)
    return s


SCRATCH = _scratch()
SEMAPHORES = (["qv", "qs", "qt", "qg", "loc", "d_pg", "d_og", "d_x", "d_u", "d_w", "d_v", "d_t", "d_o", "d_ol", "d_y0", "d_y1"]
              + ["rq%d" % r for r in range(3)] + ["ra%d" % r for r in range(3)])


def make_queue_tools(g, T):
    eng = {"v": g.vector, "s": g.scalar, "t": g.tensor, "g": g, "y": g.sync}
    own = {"v": "qv", "s": "qs", "t": "qt", "g": "qg"}
    count = {k: 0 for k in SEMAPHORES}
    known = {k: {} for k in eng}
    clock = {}
    hist = {}
    bits = {}

    def region(ref):
        name, idx = ref
        key = (name, str(idx))
        if key not in bits:
            if name == "ps":
                bits[key] = (0, 128, 1 << idx)
            else:
                shape = SCRATCH[name][1][1:]
                n = 1
                for k in shape:
                    n *= k
                a = np.arange(n).reshape(shape)
                sel = np.zeros(n, np.uint8)
                sel[a[idx[1:]].reshape(-1)] = 1
                m = int.from_bytes(np.packbits(sel, bitorder="little").tobytes(), "little")
                bits[key] = (idx[0].start or 0, idx[0].stop or 128, m)
        return bits[key]

    def learn(q, ev):
        k = known[q]
        for s, n in clock[ev].items():
            if k.get(s, 0) < n:
                k[s] = n

    def need(q, events):
        todo = [e for e in set(events) if known[q].get(e[0], 0) < e[1]]
        todo = [e for e in todo if not any(f != e and clock[f].get(e[0], 0) >= e[1] for f in todo)]
        for e in sorted(todo):
            if known[q].get(e[0], 0) < e[1]:
                eng[q].wait_ge(T.sem[e[0]], e[1])
                learn(q, e)

    def deps(q, ins, outs):
        ev = []
        for refs, write in ((ins, False), (outs, True)):
            for ref in refs:
                p0, p1, m = region(ref)
                for (h0, h1, hm, hw, hq, he) in hist.get(ref[0], ()):
                    if (hw or write or ref[0] == "ps" and hq != q) and h0 < p1 and p0 < h1 and hm & m:
                        if not hw and hq == q:
                            continue
                        ev.append(he)
        return ev

    def note(q, ev, ins, outs):
        for refs, write in ((ins, False), (outs, True)):
            for ref in refs:
                p0, p1, m = region(ref)
                lst = hist.setdefault(ref[0], [])
                if write:
                    lst[:] = [h for h in lst if not (p0 <= h[0] and h[1] <= p1 and (h[2] & ~m) == 0)]
                lst.append((p0, p1, m, write, q, ev))

    def op(q, call, outs, ins):
        need(q, deps(q, ins, outs))
        sem = own[q]
        count[sem] += 1
        ev = (sem, count[sem])
        call().then_inc(T.sem[sem], 1)
        clock[ev] = dict(known[q])
        clock[ev][sem] = count[sem]
        note(q, ev, ins, outs)

    def dmas(sem, items):
        count[sem] += 16 * len(items)
        ev = (sem, count[sem])
        clock[ev] = {sem: count[sem]}
        for q, out, in_, outs, ins in items:
            need(q, [e for e in deps(q, ins, outs) if e != ev])
            eng[q].dma_start(out, in_).then_inc(T.sem[sem], 16)
            for s, n in known[q].items():
                if clock[ev].get(s, 0) < n:
                    clock[ev][s] = n
        for q, out, in_, outs, ins in items:
            note("dma", ev, ins, outs)

    def send(call, ins, n):
        need("g", deps("g", ins, []))
        call()
        count["loc"] += n
        clock[("loc", count["loc"])] = {"loc": count["loc"]}

    def arrives(sem, n, outs):
        count[sem] += n
        ev = (sem, count[sem])
        clock[ev] = {sem: count[sem]}
        note("remote", ev, [], outs)

    def finish():
        for s in SEMAPHORES:
            if count[s] and known["g"].get(s, 0) < count[s]:
                g.wait_ge(T.sem[s], count[s])
    return op, dmas, send, arrives, finish


def rank_program(g, core, T, topo):
    rank = T.rank_of(core)
    if rank is None:
        return
    op, dmas, send, arrives, finish = make_queue_tools(g, T)
    S_ = slice
    ANY = slice(None)

    def R(name, *idx, p=slice(0, 128)):
        if name in SMALL:
            o, n = SMALL[name]
            i = idx[0] if idx else slice(0, n)
            name, idx = "sm", (slice(o + i.start, o + i.stop, i.step),)
        return (name, (p,) + tuple(idx)) if idx else (name, (p,) + tuple(ANY for _ in SCRATCH[name][1][1:]))

    def V(ref):
        return T[ref[0]][ref[1]]

    def bank(k, n):
        return T.ps[:, 512 * k:512 * k + n]

    def cp(q, out, in_, scale=None):
        if q == "v":
            op(q, lambda: g.vector.tensor_copy(V(out), V(in_)), [out], [in_])
        elif scale is None:
            op(q, lambda: g.scalar.activation(V(out), V(in_), COPY), [out], [in_])
        else:
            op(q, lambda: g.scalar.activation(V(out), V(in_), COPY, scale=V(scale)), [out], [in_, scale])

    def frombank(q, out, k, n=C, scale=None):
        if q == "v" and scale is None:
            op(q, lambda: g.vector.tensor_copy(V(out), bank(k, n)), [out], [("ps", k)])
        elif q == "v":
            op(q, lambda: g.vector.tensor_scalar(V(out), bank(k, n), scale, None, OP.mult), [out], [("ps", k)])
        elif scale is None:
            op(q, lambda: g.scalar.activation(V(out), bank(k, n), COPY), [out], [("ps", k)])
        else:
            op(q, lambda: g.scalar.activation(V(out), bank(k, n), COPY, scale=scale), [out], [("ps", k)])

    def gather(q, out, win, off):
        if q == "v":
            op(q, lambda: g.vector.tensor_copy(V(out), V(win).indirect(V(off))), [out], [win, off])
        else:
            op(q, lambda: g.scalar.activation(V(out), V(win).indirect(V(off)), COPY), [out], [win, off])

    def gather_add(out, win, off, in1):
        op("v", lambda: g.vector.tensor_tensor(V(out), V(win).indirect(V(off)), V(in1), OP.add), [out], [win, off, in1])

    def tt(out, a, b, o):
        op("v", lambda: g.vector.tensor_tensor(V(out), V(a), V(b), o), [out], [a, b])

    def ts(out, a, s1, s2, o0, o1=None):
        v1 = V(s1) if isinstance(s1, tuple) else s1
        v2 = V(s2) if isinstance(s2, tuple) else s2
        ins = [a] + [s for s in (s1, s2) if isinstance(s, tuple)]
        if o1 is None:
            op("v", lambda: g.vector.tensor_scalar(V(out), V(a), v1, None, o0), [out], ins)
        else:
            op("v", lambda: g.vector.tensor_scalar(V(out), V(a), v1, v2, o0, o1), [out], ins)

    def tr(out, in_):
        op("v", lambda: g.vector.transpose(V(out), V(in_)), [out], [in_])

    def ms(out, c):
        op("v", lambda: g.vector.memset(V(out), c), [out], [])

    def quant(oc_, op_, in_):
        op("v", lambda: g.vector.quantize_mx(V(oc_), V(op_), V(in_)), [oc_, op_], [in_])

    def mm(k, lc, lp, rc, rp, n=C):
        op("t", lambda: g.tensor.matmul_mx(bank(k, n), V(lc), V(lp), V(rc), V(rp), True, True), [("ps", k)], [lc, lp, rc, rp])

    def iota(out, pattern, base, cm, **kw):
        op("g", lambda: g.iota(V(out), pattern, base, cm, **kw), [out], [])

    def quadrant(a):
        return slice(32 * a, 32 * a + 32)

    def cols(name, a, n):
        return R(name, S_(a, a + n))

    def partner(r):
        return T.cores[rank ^ STEP[r]]

    def ways(src, dst):
        return topo.engines(src, dst)[:8]

    def remote(r, out, in_, sem, ins):
        rid, pid, _ = topo.addr(partner(r))
        e = ways(core, partner(r))
        send(lambda: g.remote_dma(out, in_, T.sem[sem], T.sem.loc, pid, rid, sum(1 << k for k in e)), ins, len(e))

    def q_of(r, a=0, n=C):
        return cols("qc%d" % r, a, n), cols("qp%d" % r, a, n)

    def send_state(r):
        remote(r, T["lc%d" % r][:].bitcast(dt.uint8), T["qc%d" % r][:].bitcast(dt.uint8), "rq%d" % r, [R("qc%d" % r)])
        remote(r, T["lp%d" % r][:], T["qp%d" % r][:], "rq%d" % r, [R("qp%d" % r)])

    for r in range(3):
        n = len(ways(partner(r), core))
        arrives("rq%d" % r, 2 * n, [R("lc%d" % r), R("lp%d" % r)])
        arrives("ra%d" % r, n, [R("zl%d" % r)])

    dmas("d_pg", [("y", T.pgi[:], T.pg[:], [R("pgi")], [])])
    dmas("d_og", [("s", T.ogi[:], T.og[:], [R("ogi")], [])])
    dmas("d_x", [("y", T.xb[:], T.x[:], [R("xb")], [])])
    dmas("d_u", [("s", T.ub[:], T.u[:], [R("ub")], [])])

    def c1(k):
        return cols("cst", k, 1)

    def ti(k):
        return cols("ti", k, 1)
    iota(R("pidx"), [[0, 1]], 0, 1)
    iota(R("wini"), [[NW, 16]], -8 * NW, 0)
    ms(R("ones"), 1.0)
    ms(cols("tab", 0, 1024), 0.0)
    for k in (TW - 2048, TW - 1024):
        cp("s", cols("tab", k, 1024), cols("tab", 0, 1024))
    ms(cols("tab", 1024, TW - 3072), 0.0)
    for b in range(4):
        o = cols("ebt", 512 * b, 512)
        op("g", lambda: g.affine_select(V(o), T.ones[:], [[-1, 512]], OP.is_equal, 0.0, b, 4), [o], [R("ones")])
    ts(ti(0), R("pidx"), 4, 1, OP.arith_shift_right, OP.bitwise_and)
    ts(ti(1), R("pidx"), 5, None, OP.arith_shift_right)
    ms(R("pgf"), 0.0)
    ts(c1(2), ti(0), 4.0, None, OP.mult)
    ts(ti(2), R("pidx"), 15, None, OP.bitwise_and)
    tt(c1(3), c1(2), ti(1), OP.add)
    ms(R("ogf"), 0.0)
    ts(c1(4), c1(3), float(NW), float(BASE), OP.mult, OP.add)

    ts(cols("pgf", 0, 24), R("pgi"), c1(4), None, OP.add)
    tr(R("pgt"), R("pgf"))
    items = []
    for G in range(6):
        for h in range(2):
            a, n = BASE + 4 * NW * h, 4 * NW
            pr = slice(16 * G, 16 * G + 1)
            items.append((("y", "s")[h], T.tab[pr, a:a + n], T.pgt[:, 16 * h:16 * h + 16],
                          [R("tab", S_(a, a + n), p=pr)], [cols("pgt", 16 * h, 16)]))
    dmas("d_t", items)
    dmas("d_w", [("y", T.wcod[:].bitcast(dt.uint8), T.wc[:], [R("wcod")], []), ("y", T.wpl[:], T.ws[:], [R("wpl")], [])])
    dmas("d_v", [("y", T.vb16[:], T.v[:], [R("vb16")], [])])

    ts(R("t24"), R("ogi"), 1, None, OP.bitwise_and)
    ts(R("t24b"), R("ogi"), 1, None, OP.arith_shift_right)
    cp("v", c1(1), ti(0))
    ts(c1(0), ti(0), -1.0, 1.0, OP.mult, OP.add)
    ts(R("t24"), R("t24"), 4.0, None, OP.mult)
    ms(R("one16"), 1.0)
    ts(c1(7), ti(1), 128.0, None, OP.mult)
    ts(c1(8), ti(0), 64.0, None, OP.mult)
    tt(cols("ogf", 0, 24), R("t24"), R("t24b"), OP.add)
    ts(ti(3), R("pidx"), 1, 3, OP.arith_shift_right, OP.bitwise_and)
    cp("v", R("win"), R("wini"))
    tt(c1(7), c1(7), c1(8), OP.add)
    tr(R("ogt"), R("ogf"))
    for h in range(2):
        ts(R("mk8", S_(h, 32, 2)), R("one16"), c1(h), 8.0, OP.mult, OP.mult)
    tt(c1(7), c1(7), ti(2), OP.add)
    ms(cols("win", 0, 1), 0.0)

    def spread(src, xd, xw, nsrc):
        for H in range(2):
            for h in range(2):
                cp("vs"[H], cols(xd, 32 * h + 16 * H, 16), cols(src, 16 * h, 16))
        k = 0
        for a in range(nsrc):
            for b in range(4):
                cp("vs"[k % 2], R(xw, S_(64 * a, 64 * a + 64), p=quadrant(b)), R(xd, p=quadrant(a)))
                k += 1

    spread("ogt", "oxd", "oxw", 4)
    for s in range(4):
        ts(cols("js", s, 1), c1(7), 16.0 * s + BASE, None, OP.add)
    cp("v", cols("idxf", 56, 8), cols("mk8", 0, 8))
    for h in range(2):
        ts(R("jbm", S_(h, 8, 2)), R("js"), c1(h), None, OP.mult)
    ts(ti(4), R("pidx"), 3, 1, OP.arith_shift_right, OP.bitwise_and)
    ts(c1(9), ti(3), 32.0, None, OP.mult)
    ts(c1(10), ti(4), 16.0, None, OP.mult)
    tr(R("ox"), R("oxw"))
    tt(c1(9), c1(9), c1(10), OP.add)
    ts(R("selu"), cols("one16", 0, 10), c1(9), None, OP.mult)
    for par, name in ((0, "oe"), (1, "oo")):
        for a in range(4):
            for h in range(2):
                o = R(name, S_(h, 32, 2), p=quadrant(a))
                i = R("ox", ANY, par, S_(8 * a + 4 * h, 8 * a + 4 * h + 4), p=quadrant(a))
                s = R("cst", S_(h, h + 1), p=quadrant(a))
                if par:
                    cp("s", o, i, s)
                else:
                    ts(o, i, s, None, OP.mult)
    oe, oo, mk8 = R("oe"), R("oo"), R("mk8")
    IE, IO = cols("idxf", 0, 32), cols("idxf", 32, 24)
    tt(R("dd"), oo, oe, OP.subtract)
    tt(IO, cols("oe", 8, 24), cols("oo", 0, 24), OP.subtract)
    tt(IE, R("dd"), mk8, OP.add)
    tt(IO, IO, cols("mk8", 0, 24), OP.add)
    cp("v", R("idxu"), R("idxf"))
    ts(R("off0"), cols("oe", 0, 8), float(NW), None, OP.mult)
    tt(R("off0"), R("off0"), R("jbm"), OP.add)
    cp("v", cols("offu", 0, 8), R("off0"))

    KAP = [0, 4, 1, 5, 2, 6, 3, 7]

    def rep(k):
        gather("s", cols("rep", 128 * KAP[k], 128), R("win"), cols("idxu", 8 * KAP[k], 8))

    def walk(first, fill):
        for k in range(first, 8):
            z = KAP[k]
            blk, off = (128 * z, 128), cols("offu", 8 * z, 8)
            if k < 7:
                gather_add(cols("wk", *blk), R("tab"), off, cols("rep", *blk))
                pause(fill)
            else:
                gather("v", cols("wk", *blk), R("tab"), off)
                early_addresses(2)
            tr(cols("tt", *blk), cols("wk", *blk))
            if k < 6:
                pause(fill)
            elif k == 6:
                early_addresses(0)
            if k < 7:
                cp("v", cols("offu", 8 * KAP[k + 1], 8), R("tt", S_(128 * z, 128 * z + 128, 16)))
                if k == 6:
                    early_addresses(1)
                else:
                    pause(fill)

    def pause(fill):
        if fill:
            fill.pop(0)()

    def differences():
        return [lambda: tt(R("dv"), R("idxf", S_(0, 64, 2)), R("idxf", S_(1, 64, 2)), OP.add),
                lambda: ts(R("dv"), R("dv"), -float(NW), 8.0 * NW, OP.mult, OP.add)]

    def early_addresses(step):
        if step == 0:
            tt(cols("vs", 0, 28), R("tt", S_(0, 896, 32)), R("tt", S_(16, 896, 32)), OP.add)
        elif step == 1:
            tt(cols("vs", 0, 28), cols("vs", 0, 28), cols("dv", 0, 28), OP.add)
        else:
            for s in range(4):
                cp("v", R("vadr", S_(8 * s, 8 * s + 7)), R("vs", S_(s, 28, 4)))

    def last_address():
        tt(R("vadr", S_(7, 32, 8)), R("tt", S_(896, 1024, 32)), R("tt", S_(912, 1024, 32)), OP.add)

    def list_of_addresses():
        ts(cols("eb", 0, 28), cols("vs", 0, 28), -float(BASE), None, OP.add)
        ts(cols("eb", 28, 4), R("vadr", S_(7, 32, 8)), -float(BASE), None, OP.add)

    def tt8(k):
        return R("tt", S_(128 * KAP[k], 128 * KAP[k] + 128, 16))

    def ahead(k, even):
        w = 32 if even else 24
        src = IE if even else IO
        s0, s1 = R("tts", S_(0, 128, 16)), R("tts", S_(128, 256, 16))
        nxt = cols("idxf", 8 * KAP[k + 1], 8)
        return [
            lambda: tt(cols("dd", 0, w), src, cols("mk8", 0, w), OP.subtract),
            lambda: (ts(R("d0"), cols("dd", 0, 8), float(NW), None, OP.mult), tt(R("idxs"), cols("mk8", 0, 8), cols("dd", 0, 8), OP.subtract)),
            lambda: (tt(R("offsf"), R("off0") if even else tt8(0), R("d0"), OP.add), cp("v", R("idxsu"), R("idxs"))),
            lambda: (cp("v", cols("offs", 0, 8), R("offsf")), gather("s", R("reps"), R("win"), R("idxsu"))),
            lambda: gather_add(cols("wks", 0, 128), R("tab"), cols("offs", 0, 8), R("reps")),
            lambda: tr(cols("tts", 0, 128), cols("wks", 0, 128)),
            lambda: cp("v", cols("offs", 8, 8), s0),
            lambda: gather("v", cols("wks", 128, 128), R("tab"), cols("offs", 8, 8)),
            lambda: tr(cols("tts", 128, 128), cols("wks", 128, 128)),
            lambda: (tt(R("yk"), nxt, cols("mk8", 0, 8), OP.subtract), tt(R("yt"), s1, tt8(k + 1), OP.subtract),
                     ts(cols("dd2", 0, w), cols("dd", 0, w), -2.0, None, OP.mult)),
            lambda: (tt(R("yk"), R("yk"), cols("dd", 0, 8), OP.add), tt(R("y0"), s0, tt8(k), OP.subtract)),
            lambda: (ts(R("yk"), R("yk"), float(NW), None, OP.mult), ts(R("t3"), cols("dd", 8, 8), float(NW), None, OP.mult)),
            lambda: tt(R("y1"), R("yt"), R("yk"), OP.add),
        ]

    def select(k):
        tr(R("xx" + k), R("xw" + k))
        ts(R("cl" + k), R("xx" + k), c1(4), c1(5), OP.max, OP.min)

    def totals(k):
        op("v", lambda: g.vector.tensor_tensor_scan(V(R("sc" + k)), V(R("zm")), V(R("cl" + k)), 0.0, OP.mult, OP.add),
           [R("sc" + k)], [R("zm"), R("cl" + k)])

    def scores(r, x, a, n, q, k):
        mm(k, cols("uc", 2 * x, 128), cols("upl", 2 * x, 128), *q_of(r, a, n), n)
        frombank(q, cols("sct", NW * x + a, n), k, n)

    def unpack(c, p, banks):
        for b in range(4):
            mm(banks + b, cols("ec", 128 * b, 128), cols("ep", 128 * b, 128), R(c), R(p))

    for k in range(7):
        rep(k)

    def first_state():
        quant(*q_of(0), R("xb"))
        send_state(0)
        for x in range(8):
            iota(cols("sct", NW * x + C, NW - C), [[0, NW - C]], 0, 0, allow_small_or_imprecise_dtypes=True)

    def scoring_columns():
        op("v", lambda: g.vector.tensor_copy(T.uc[:].bitcast(dt.uint32), T.uq0[:].bitcast(dt.uint32).indirect(T.selu[:])),
           [R("uc")], [R("uq0"), R("selu")])
        op("s", lambda: g.scalar.activation(T.upl[:], T.up0[:].indirect(T.selu[:]), COPY), [R("upl")], [R("up0"), R("selu")])
    aim = ahead(0, True)
    fill = aim[:4] + [lambda: quant(R("uq0"), R("up0"), R("ub")), first_state, scoring_columns] + differences() + aim[4:] + [
        lambda: ms(R("zm"), 1.0),
        lambda: ms(R("zm", S_(0, 192, 8)), 0.0),
        lambda: ts(c1(5), c1(4), float(NW), None, OP.add),
        lambda: ts(c1(6), c1(3), 7.0 * NW, 7.0 * NW + 8 * BASE, OP.mult, OP.add)]
    walk(0, fill)
    for x in range(8):
        scores(0, x, 0, C, "s", x)
    last_address()
    list_of_addresses()

    for r in range(3):
        odd = r == 1
        for k in range(2):
            gather("vs"[k], cols("ev", 256 * k, 256), R("sct"), cols("eb", 16 * k, 16))
        while fill:
            pause(fill)
        if r == 0:
            quant(R("ec"), R("ep"), R("ebt"))
        unpack("qc%d" % r, "qp%d" % r, 0)
        for b in range(3):
            frombank("s", cols("fb", C * b, C), b)
        n = 12 if odd else 16
        if odd:
            tt(cols("bt", 0, 192), cols("ev", 256, 192), cols("ev", 64, 192), OP.is_gt)
        else:
            tt(R("bt"), cols("ev", 0, 256), cols("ev", 256, 256), OP.is_gt)
        for h in range(2):
            ts(R("bd", S_(0, n), h, ANY), cols("bt", 0, 16 * n), c1(h), None, OP.mult)
        tr(cols("btt", 0, 32 * n), R("bd", S_(0, n), ANY, ANY))
        bm, bm0, bm1 = R("btt", S_(0, 32 * n, 16)), R("btt", S_(0, 128, 16)), R("btt", S_(128, 256, 16))
        m, m2 = cols("mm", 0, 2 * n), cols("mm2", 0, 2 * n)
        mine = IO if odd else IE
        first = 1 if odd else 0
        t0, t1, t2 = tt8(0), tt8(first), tt8(first + 1)
        tt(m2, bm, cols("dd2", 0, 2 * n), OP.mult)
        tt(R("t1"), bm0, R("y1"), OP.mult)
        tt(R("t2"), bm1, R("t3"), OP.mult)
        tt(mine, mine, m2, OP.add)
        tt(t2, t2, R("t1"), OP.add)
        tt(m, bm, cols("dd", 0, 2 * n), OP.mult)
        if odd:
            cp("v", cols("idxu", 32, 24), IO)
        else:
            cp("v", cols("idxu", 0, 32), IE)
        tt(t2, t2, R("t2"), OP.add)
        rep(first + 2)
        a, k = (0, 32) if odd else (32, 24)
        if odd:
            tt(cols("idxf", 0, 24), cols("idxf", 0, 24), m, OP.add)
        else:
            tt(IO, IO, cols("mm", 8, 24), OP.add)
        cp("v", cols("offu", 8 * KAP[first + 2], 8), t2)
        if odd:
            tt(cols("idxf", 8, 24), cols("idxf", 8, 24), m, OP.add)
        else:
            tt(IO, IO, cols("mm", 0, 24), OP.add)
        tt(R("m0"), bm0, R("d0"), OP.mult)
        cp("v", cols("idxu", a, k), cols("idxf", a, k))
        for k in range(first + 3, 7):
            rep(k)
        up, dn = (OP.subtract, OP.add) if odd else (OP.add, OP.subtract)
        E, O = (cols("oe", 8, 24), cols("oo", 0, 24)) if odd else (oe, oo)
        f0 = t0 if odd else R("off0")
        diff = differences()
        fill = [lambda: (tt(R("y0"), bm0, R("y0"), OP.mult), tt(f0, f0, R("m0"), OP.add)), lambda: (tt(t1, t1, R("y0"), OP.add), diff[0]())]
        fill += ahead(0 if odd else 1, odd) if r < 2 else []
        orders = lambda: (tt(O, O, m, dn), tt(E, E, m, up))
        fill.insert(3, lambda: (diff[1](), orders()))
        if r == 0:
            fill.append(lambda: quant(R("vq"), R("vp"), R("vb16")))
        walk(first + 2, fill)
        last_address()
        tr(R("ltA"), R("vadr"))
        list_of_addresses()
        spread("ltA", "xdA", "xwA", 3)
        gather("s", R("brep"), cols("tab", BASE, TW - BASE), R("eb"))
        select("A")
        totals("A")
        ts(R("al%d" % r), R("scA", S_(7, 192, 8)), c1(6), None, OP.subtract)
        remote(r, T["zl%d" % r][:], T["al%d" % r][:], "ra%d" % r, [R("al%d" % r)])
        unpack("lc%d" % r, "lp%d" % r, 4)
        for b in range(2):
            frombank("s", cols("dp", C * b, C), 4 + b)
        tr(R("brt"), R("brep"))
        for k in range(4):
            cp("v", cols("lb", 8 * k, 8), R("brt", S_(16 * k, 512, 64)))
        tr(R("ltB"), R("lb"))
        spread("ltB", "xdB", "xwB", 3)
        for b in range(2, 4):
            frombank("s", cols("dp", C * b, C), 4 + b)
        select("B")
        if r == 2:
            tt(cols("olf", 0, 16), R("oe", S_(0, 32, 2)), R("oe", S_(1, 32, 2)), OP.add)
            tt(cols("olf", 16, 16), R("oo", S_(0, 32, 2)), R("oo", S_(1, 32, 2)), OP.add)
            ts(R("olg"), R("olf"), 4.0, -7.0, OP.is_ge, OP.mult)
            tt(R("olf"), R("olf"), R("olf"), OP.add)
            tt(R("olf"), R("olf"), R("olg"), OP.add)
            tr(R("olt"), R("olf"))
            items = []
            for a in range(3):
                for par in range(2):
                    for h in range(2):
                        p = slice(32 * a + 16 * par, 32 * a + 16 * par + 16)
                        c = 128 * a + 64 * h
                        items.append(("y", T.ol[par:8:2, c:c + 64], T.olt[p, 16 * h:16 * h + 16], [], [R("olt", S_(16 * h, 16 * h + 16), p=p)]))
            dmas("d_ol", items)
        zt, zc, zp = "zt%d" % r, "zc%d" % r, "zp%d" % r
        for h in range(2):
            for b in (0, 2, 1, 3):
                gather("vs"[b // 2], R(zt, S_(4 * HC * h + b, 4 * HC * (h + 1), 4)), cols("dp", C * b, C), cols("zl%d" % r, 12 * h, 12))
        totals("B")
        for h in range(2):
            quant(cols(zc, HC * h, HC), cols(zp, HC * h, HC), cols(zt, 4 * HC * h, 4 * HC))
        for k in range(4):
            for l in range(2):
                ts(R("bl", S_(4 * (k & 1) + (k & 2) + l, 24, 8)), R("scB", S_(32 * l + 8 * k + 7, 192, 64)), c1(6), None, OP.subtract)
        for h in range(2):
            mm(h, cols("wcod", 0, 128), cols("wpl", 0, 128), cols(zc, HC * h, HC), cols(zp, HC * h, HC), HC)
            frombank("sv"[h], cols("rs", HC * h, HC), h, HC, 0.03125)
        nx = "xs%d" % (r + 1)
        for b, k in ((1, 2), (3, 5), (2, 4)):
            mm(k, cols("wcod", 128 * b, 128), cols("wpl", 128 * b, 128), R(zc), R(zp))
            frombank("s", cols("rs", C * b, C), k, C, 0.03125)
        for h in range(2):
            gather("s", cols("gs", HC * h, HC), cols("rs", 3 * C, C), cols("bl", 12 * h, 12))
        for h in range(2):
            for b in range(3):
                gather_add(R(nx, S_(4 * HC * h + b, 4 * HC * (h + 1), 4)), cols("rs", C * b, C), cols("bl", 12 * h, 12), cols("fb", C * b + HC * h, HC))
            o, i = R(nx, S_(4 * HC * h + 3, 4 * HC * (h + 1), 4)), cols("gs", HC * h, HC)
            op("v", lambda: g.vector.tensor_tensor(V(o), V(i), T.ps[:, 512 * 3 + HC * h:512 * 3 + HC * h + HC], OP.add), [o], [i, ("ps", 3)])
            quant(*q_of(r + 1, HC * h, HC), cols(nx, 4 * HC * h, 4 * HC))
            if r < 2:
                for x in range(8):
                    if h == 0:
                        scores(r + 1, x, 0, HC, "s", (0, 1, 2, 6, 7, 5, 4, 0)[x])
                    else:
                        scores(r + 1, x, HC, HC, "sv"[x % 2], x)
                        pause(fill)
            else:
                mm(h, R("vq"), R("vp"), *q_of(3, HC * h, HC), HC)
                frombank("sv"[h], cols("ys", HC * h, HC), h, HC)
                dmas("d_y%d" % h, [("y", T.y[:, HC * h:HC * h + HC], T.ys[:, HC * h:HC * h + HC], [], [cols("ys", HC * h, HC)])])
        while fill:
            pause(fill)
        if r < 2:
            send_state(r + 1)

    qc, qp = q_of(3)
    dmas("d_o", [("s", T.oc[:], T.qc3[:].bitcast(dt.uint8), [], [qc])]
         + [(("s", "y")[k % 2], T.osc[4 * k:4 * k + 4, :], T.qp3[32 * k:32 * k + 4, :], [], [qp]) for k in range(4)])
    finish()
